import numpy as np, ml_dtypes
CORES = [23,119,17,113]
N = 4
import mx_ref
BF = ml_dtypes.bfloat16
def gentries(a):
    return np.ascontiguousarray(a.reshape(8, 16, -1).transpose(0, 2, 1)).reshape(8, -1)
def gtable(e):
    e = np.asarray(e); return np.ascontiguousarray(e.reshape(8, -1, 16).transpose(0, 2, 1)).reshape(128, -1).astype(np.int32)
def gcols(t, e):
    v = np.concatenate([t.reshape(8, 16, -1, 4), np.zeros((8, 16, 1, 4), BF)], axis=2)
    return np.ascontiguousarray(np.stack([v[g][:, e[g]] for g in range(8)])).reshape(128, -1)
def tile(rs):
    return np.stack(rs, axis=2).reshape(128, -1).astype(BF)
def pick(q, e):
    c = np.concatenate([q[0].reshape(128, -1, 4), np.zeros((128, 1, 4), np.uint8)], axis=1); s = np.concatenate([q[1], np.ones((16, 1), np.uint8)], axis=1)
    return (np.ascontiguousarray(c[:, e].reshape(128, -1)), np.ascontiguousarray(s[:, e]))
def join(*qs):
    return (np.concatenate([q[0] for q in qs], axis=1), np.concatenate([q[1] for q in qs], axis=1))
def put(q, e, v):
    c, s = q[0].reshape(128, -1, 4).copy(), q[1].copy(); c[:, e] = v[0].reshape(128, -1, 4); s[:, e] = v[1]
    return (c.reshape(128, -1), s)
def pk(c, s):
    return (np.ascontiguousarray(c), mx_ref.live(s))
def emit(q):
    return q[0], q[1]
def packed(v, rng):
    q = [mx_ref.quantize(np.ascontiguousarray(v[r])) for r in range(N)]
    return np.stack([a for a, b in q]), np.stack([mx_ref.plane(b, rng) for a, b in q])
def values_of_codes():
    e, c = np.zeros((128, 128, 4), np.float32), np.zeros((128, 2, 4), np.uint8)
    e[np.arange(128), np.arange(128), 0] = 1
    c[:127, :, 0] = np.arange(256).reshape(2, 128).T[:127]
    return mx_ref.matmul(mx_ref.quantize(e.reshape(128, 512).astype(BF)), (c.reshape(128, 8), np.full((16, 2), 127, np.uint8))).T.reshape(-1).astype(np.float64)
CODE_VALUE, SCALE_VALUE = values_of_codes(), 2.0 ** (np.arange(256) - 127.0)
def decode(q):
    return (CODE_VALUE[q[0]].reshape(16, 8, -1, 4) * SCALE_VALUE[q[1]][:, None, :, None] + 0.0).reshape(128, -1).astype(np.float32)
def f(rng, *shape):
    return mx_ref.flush((rng.standard_normal(shape, dtype=np.float32) * np.exp2(rng.integers(-2, 3, shape[:-1] + (1,)))).astype(BF))
def wide(rng, *shape, cols=0):
    v = rng.standard_normal(shape, dtype=np.float32) * np.exp2(rng.integers(-12, 13, shape)).astype(np.float32)
    if cols: v *= np.repeat(np.exp2(rng.integers(-cols, cols + 1, shape[:-2] + (1, shape[-1] // 4))) * (rng.random(shape[:-2] + (1, shape[-1] // 4)) > 0.0625), 4, axis=-1).astype(np.float32)
    return mx_ref.flush(v.astype(BF))
C = 384
STEP = [1, 2, 3]
GAPS = [[2, 4, 5, 6, 7, 8], [3, 4, 5, 6, 7, 8]]
def numbers_of(rng):
    return {"x": np.array(f(rng, N, 128, 4 * C)), "u": np.array(f(rng, N, 128, 512)), "v": np.array(f(rng, N, 128, 512))}
def full(rng, k):
    h = 128 + rng.permutation(128)[:k]
    low = rng.permutation(np.concatenate([2 * h, 2 * h + 1]))[:C - 127 - k]
    return np.sort(np.concatenate([np.arange(1, 128), h, low]))
def below(h):
    return np.concatenate([np.arange(h << n, (h + 1) << n) for n in range(10 - h.bit_length())])
def lean(side, slot):
    c = 3 - side
    return np.sort(np.concatenate([[1], below(2 + side), np.concatenate([[c], below(2 * c + slot)])[:C - 256]]))
def ragged(rng, first):
    cuts, left = [], 511 - C
    for n, most in [(n, 1) for n in first] + [(n, 9) for n in range(3, 9)]:
        size = 2 ** (9 - n) - 1
        k = min(most, left // size)
        cuts += [n] * k
        left -= k * size
    keep = np.arange(512) > 0
    for n in sorted(cuts):
        h = np.arange(2 ** n, 2 ** (n + 1))
        h = int(rng.choice(h[keep[h] & keep[h ^ 1]]))
        keep[below(h)] = False
    return np.flatnonzero(keep)
def grown(h, places):
    at = np.zeros(512, np.int64)
    at[h] = places
    e = np.zeros(C, np.int64)
    e[places[1:]] = 2 * at[h[1:] >> 1] + (h[1:] & 1)
    return e
def shuffled(rng):
    return np.concatenate([[0], 1 + rng.permutation(C - 1)])
def trees(rng):
    t = np.stack([np.stack([grown(full(rng, int(rng.integers(112, 129))), shuffled(rng)) for g in range(8)]) for r in range(N)])
    o = rng.permutation(8)
    for r in range(N):
        for n in range(2): t[r, o[(r + 4 * n) % 8]] = grown(ragged(rng, GAPS[n]), shuffled(rng))
    return t
def stored(t):
    return {"se": np.stack([gtable(t[r]) for r in range(N)])}
def weights(rng, w):
    c, s = packed(np.ascontiguousarray(w).reshape(N, 128, 2048), rng)
    return {"wc": c, "ws": s}
def layers(rng, still=[], pairs=False):
    w = np.array(f(rng, N, 128, 2048)).reshape(N, 8, 16, 4, 8, 16, 4)
    for i in still:
        w[:, :, i] = 0
        w[:, :, :, :, :, i] = 0
    if pairs:
        w[:, :, :, :, :, 8:] = 0
        for g in range(8):
            w[:, g, 8, 0, g, 8, 0] = -28.0
            for b in range(4): w[:, g, 10, b, g, 9, 0] = -2.0 ** (b - 5)
    return weights(rng, w)
def setup_inputs(rng):
    return {**numbers_of(rng), **stored(trees(rng)), **layers(rng)}
def setup_inputs_ties(rng):
    d = numbers_of(rng)
    o = rng.permutation(N)
    k = rng.integers(-1, 2, (N, 8, C)).astype(np.float32)
    k[o[1]] = -1
    x = d["x"].reshape(N, 8, 16, C, 4)
    x[:, :, 0] = 0
    x[:, :, 0, :, 0] = k.astype(BF)
    a = np.exp2(rng.integers(-3, 4, (1, 8, 1)).astype(np.float32))
    x[:, :, 8:] = 0
    x[:, :, 8, :, 0] = (-1.125 * a).astype(BF)
    x[:, :, 10, :, 0] = (-0.0703125 * a).astype(BF)
    c = np.ones(N, np.float32)
    c[o[0]] = 0
    c[o[2]] = -1
    u = d["u"].reshape(N, 128, 128, 4)
    u[:, :, ::16] = 0
    for h in range(0, 128, 16): u[:, h, h, 0] = c.astype(BF)
    return {"x": x.reshape(N, 128, 4 * C), "u": u.reshape(N, 128, 512), "v": d["v"], **stored(trees(rng)), **layers(rng, [0], True)}
def setup_inputs_near(rng):
    d = numbers_of(rng)
    o = rng.permutation(N) % 2
    k = np.where(o == 0, 2.0 ** -30, 1.0).astype(np.float32)
    x = np.zeros((N, 8, 16, C, 4), np.float32)
    s = rng.integers(-1, 2, (N, 8, C)) * k[:, None, None]
    x[:, :, 0, :, 0] = 1.125 * s
    x[:, :, 1, :, 0] = -1.25 * s
    s = rng.choice([-1.0, 1.0], (N, 8, C)) * 2.0 ** -30
    x[:, :, 8, :, 0] = 1.125 * s
    x[:, :, 9, :, 0] = -1.25 * s
    x[:, :, 2, :, 0] = 2.0 ** -28
    x[:, :, 10, :, 0] = 2.0 ** -28
    for r in range(N):
        at = [0, C - 1, int(rng.integers(C)), int(rng.integers(C))]
        for g, j in zip(rng.permutation(8)[:4], at): x[r, g, 0, j, 0] = 2.0 ** 30 * rng.choice([-1.0, 1.0])
    u = d["u"].astype(np.float32).reshape(N, 128, 128, 4)
    u[:, :, ::16] = 0
    w = np.zeros((N, 128, 4, 128, 4), np.float32)
    for h in range(0, 128, 16):
        u[:, h, h, 0] = 1.125 * k
        u[:, h + 1, h, 0] = k
        w[:, h + 8, 0, h, 0] = 0.5
        w[:, h + 9, 0, h + 1, 0] = 0.5
        w[:, h + 10, 0, h + 2, 0] = 32.0
        w[:, h + 10, 0, h + 10, 0] = 32.0
    return {"x": x.reshape(N, 128, 4 * C).astype(BF), "u": u.reshape(N, 128, 512).astype(BF), "v": d["v"], **stored(trees(rng)), **weights(rng, w.astype(BF))}
def setup_inputs_odd(rng):
    d = numbers_of(rng)
    x = (1.0 + (2 * rng.integers(0, 64, (N, 16, 8, C, 4)) + 1) * 2.0 ** -7) * np.exp2(-rng.integers(0, 7, (N, 16, 8, C, 4)).astype(np.float64)) * rng.choice([-1.0, 1.0], (N, 16, 8, C, 4))
    x[:, :, 0, :, 0] = 1.96875 * 2.0 ** 8 * rng.choice([-1.0, 1.0], (N, 16, C))
    e = rng.choice([-1.0, 1.0], (N, 8, C)) * 2.0 ** -5
    x[:, ::2, 1, :, 0] = 1.125 * e
    x[:, ::2, 2, :, 0] = -e
    u = d["u"].reshape(N, 128, 128, 4)
    u[:, :, ::16] = 0
    for h in range(0, 128, 16): u[:, h + 1:h + 3, h, 0] = 1
    return {"x": x.astype(np.float32).reshape(N, 128, 4 * C).astype(BF), "u": u.reshape(N, 128, 512), "v": d["v"], **stored(trees(rng)), **layers(rng, [0, 8])}
def setup_inputs_ends(rng):
    d = numbers_of(rng)
    o, e = rng.permutation(N) % 4, rng.permutation(N) % 4
    x = np.zeros((N, 128, C, 4))
    u = d["u"].astype(np.float32).reshape(N, 128, 128, 4)
    v = d["v"].astype(np.float32)
    w = np.zeros((N, 128, 4, 128, 4), np.float32)
    t = np.zeros((N, 8, C), np.int64)
    i = np.arange(128)
    last = i % 16 == 15
    for r in range(N):
        h = rng.permutation(8)
        c = np.where(h < 2, 0.0, h % 2 * 2.0 - 1.0)[None, :, None]
        a = -(0.9 + 0.1 * rng.random((128, C, 4))) * 2.0 ** 30
        if o[r] == 1: a = a * rng.choice([-1.0, 1.0], (C, 1))
        if o[r] == 2: a = -(1.0 + 0.125 * rng.integers(0, 8, (128, C, 4))) * 2.0 ** -30
        if o[r] == 3: a = d["x"][r].astype(np.float32).reshape(128, C, 4)[:, :1]
        x[r] = a
        if o[r] < 2:
            x[r, last] = 2.0 ** -30
            u[r, :, ::16] = c * (0.9 + 0.1 * rng.random((128, 8, 4))) * 2.0 ** 30
            v[r] = rng.choice([-1.0, 1.0], (128, 512)) * (0.9 + 0.1 * rng.random((128, 512))) * 2.0 ** 30
        if o[r] == 2:
            u[r, :, ::16] = c * (1.0 + 0.125 * rng.integers(0, 8, (128, 8, 4))) * 2.0 ** -30
            v[r] = rng.choice([-1.0, 1.0], (128, 512)) * (1.0 + 0.125 * rng.integers(0, 8, (128, 512))) * 2.0 ** -30
        if o[r] == 3: u[r, :, ::16] *= np.abs(c).astype(np.float32)
        k = np.where(last, [32.0, 32.0, 256.0, 2.0 ** -8][o[r]], 32.0)
        for b in range(4): w[r, i, b, i, b] = k
        for g in range(8):
            if e[r] == 0: t[r, g] = grown(lean(0, g % 2), np.arange(C))
            if e[r] == 1: t[r, g] = grown(lean(1, g % 2), np.concatenate([[0], np.arange(C - 1, 0, -1)]))
            if e[r] >= 2: t[r, g] = grown(ragged(rng, GAPS[g - 6]) if g >= 6 else full(rng, 128 if e[r] == 2 else (C - 125) // 3), shuffled(rng))
    return {"x": x.astype(np.float32).reshape(N, 128, 4 * C).astype(BF), "u": u.reshape(N, 128, 512).astype(BF), "v": v.astype(BF), **stored(t), **weights(rng, w.astype(BF))}
def setup_inputs_spread(rng):
    d = setup_inputs(rng)
    d["x"] = wide(rng, N, 128, 4 * C, cols=6)
    return d
def check_inputs(d):
    b = []
    for k in ("x", "u", "v"):
        a = np.abs(d[k].astype(np.float32))
        if not (np.isfinite(a).all() and ((a == 0) | (a >= 2.0 ** -30) & (a <= 2.0 ** 30)).all()): b.append("a value of " + k)
    e = np.stack([gentries(d["se"][r]) for r in range(N)])
    if not ((e >= 0) & (e < 2 * C)).all(): b.append("an entry of se")
    else:
        if e[:, :, 0].any(): b.append("se: entry 0")
        if (np.diff(np.sort(e[:, :, 1:], axis=2), axis=2) == 0).any(): b.append("se: equal seats")
        a = e >> 1
        for n in range(7): a = np.take_along_axis(e >> 1, a, 2)
        if a.any(): b.append("se: a place from which eight steps don't lead to place 0")
    none, least, most = [emit(mx_ref.quantize(np.full((128, 16), k, np.float32).astype(BF)))[1][0, 0] for k in (0.0, 2.0 ** -8, 2.0 ** 8)]
    for r in range(N):
        if ((d["wc"][r] == 0x7F) | (d["wc"][r] == 0xFF)).any(): b.append("wc: a code that is no number")
        s = mx_ref.live(d["ws"][r])
        if ((s != none) & ((s < least) | (s > most))).any(): b.append("ws: a scale out of range")
        if (((d["wc"][r].reshape(16, 8, 512, 4) & 0x7F) != 0) & (s == none)[:, None, :, None]).any(): b.append("wc: a code other than zero under the scale of zeros")
    return b
def reference(x, u, v, se, wc, ws):
    qu = [mx_ref.quantize(u[r]) for r in range(N)]
    lay = [pk(wc[r], ws[r]) for r in range(N)]
    seat = [gentries(se[r]).astype(np.int64) for r in range(N)]
    par = [seat[r] >> 1 for r in range(N)]
    now = [x[r] for r in range(N)]
    y, im = np.zeros((N, 128, C), np.float32), np.zeros((N, 8, C), np.float32)
    oc, osc = np.zeros((N, 128, 4 * C), np.uint8), np.zeros((N, 16, C), np.uint8)
    for step in STEP:
        q = [mx_ref.quantize(now[r]) for r in range(N)]
        layered, child = [], []
        for r in range(N):
            layered.append(tile([mx_ref.matmul(pick(lay[r], np.arange(128 * b, 128 * b + 128)), q[r]) * np.float32(0.03125) for b in range(4)]))
            turn = (mx_ref.matmul(qu[r], q[r])[::16] < 0).astype(np.int64)
            seat[r] = seat[r] ^ np.take_along_axis(turn, par[r], 1)
            c = np.full((8, 2 * C), -1, np.int64)
            np.put_along_axis(c, seat[r][:, 1:], np.tile(np.arange(1, C), (8, 1)), 1)
            child.append(c)
        for r in range(N):
            p = r ^ step
            m = np.zeros((8, C), np.int64)
            for depth in range(8):
                at = np.take_along_axis(m, par[r], 1)
                c = np.take_along_axis(child[p], 2 * at + (seat[r] & 1), 1)
                m = np.where(c < 0, at, c)
                m[:, 0] = 0
            e = mx_ref.quantize(gcols(layered[p], m))
            above = gcols(decode(q[r]).astype(BF), par[r]).astype(np.float32)
            now[r] = ((decode(e) + above) * np.float32(0.5)).astype(BF)
            im[r] = m
    for r in range(N):
        z = mx_ref.quantize(now[r])
        y[r] = mx_ref.matmul(mx_ref.quantize(v[r]), z)
        oc[r], osc[r] = emit(z)
    return {"y": y, "im": im, "oc": oc, "osc": osc}

@@ -1,0 +1,495 @@
+from concourse.bass import DstId, RemoteDMATransfer
+from concourse.mybir import dt, AluOpType, AxisListType, ActivationFunctionType as AF
+
+C = 384
+CH = [(0, 192), (192, 384)]
+FQ = ["AAAA", "VVVA", "VVVA"]
+SCRATCH = {
+    "KX": ("sbuf", [128, 32], "int32"), "KF": ("sbuf", [128, 32], "float32"), "tm": ("sbuf", [128, 128], "int32"),
+    "AD": ("sbuf", [128, 8], "float32"), "rL": ("sbuf", [128, 16], "float32"), "rA": ("sbuf", [128, 16], "float32"),
+    "rK": ("sbuf", [128, 16], "float32"), "rN": ("sbuf", [128, 8], "float32"), "bh": ("sbuf", [128, 16], "float32"),
+    "eqm": ("sbuf", [128, 16], "float32"), "sx": ("sbuf", [128, 16], "float32"), "ow": ("sbuf", [128, 16], "float32"),
+    "NK": ("sbuf", [128, 8], "float32"), "OH": ("sbuf", [128, 4], "float32"), "H2": ("sbuf", [128, 2], "float32"),
+    "iC": ("sbuf", [128, 512], "bfloat16"), "mk": ("sbuf", [128, 512], "bfloat16"), "R0": ("sbuf", [128, 512], "bfloat16"),
+    "TB": ("sbuf", [128, 256], "float32"), "TM": ("sbuf", [128, 256], "float32"), "TS": ("sbuf", [128, 256], "float32"),
+    "PL": ("sbuf", [128, 16], "uint16"), "PS": ("sbuf", [128, 128], "bfloat16"), "Ye": ("sbuf", [128, 32], "float32"),
+    "s5": ("sbuf", [128, 96], "float32"), "ULi": ("sbuf", [128, 8], "int32"),
+    "UL": ("sbuf", [128, 8], "uint16"), "JC": ("sbuf", [128, 32], "float32"), "hf": ("sbuf", [128, 128], "bfloat16"),
+    "idn": ("sbuf", [128, 128], "bfloat16"), "EB": ("sbuf", [128, 2048], "bfloat16"),
+    "eq": ("sbuf", [128, 512], "float8_e4m3fn_x4"), "es": ("sbuf", [128, 512], "uint8"),
+    "seI": ("sbuf", [128, 24], "int32"), "paI": ("sbuf", [128, 24], "int32"), "paU": ("sbuf", [128, 24], "uint16"),
+    "stU": ("sbuf", [128, 24], "uint16"), "xb": ("sbuf", [128, 1536], "bfloat16"), "ub": ("sbuf", [128, 512], "bfloat16"),
+    "vb": ("sbuf", [128, 512], "bfloat16"), "wq": ("sbuf", [128, 512], "float8_e4m3fn_x4"), "wp": ("sbuf", [128, 512], "uint8"),
+    "uq": ("sbuf", [128, 128], "float8_e4m3fn_x4"), "us": ("sbuf", [128, 128], "uint8"),
+    "upq": ("sbuf", [128, 128], "float8_e4m3fn_x4"), "ups": ("sbuf", [128, 128], "uint8"),
+    "vq": ("sbuf", [128, 128], "float8_e4m3fn_x4"), "vs": ("sbuf", [128, 128], "uint8"),
+    "Nc": ("sbuf", [128, 784], "bfloat16"), "LT": ("sbuf", [128, 8], "uint16"), "LL": ("sbuf", [128, 32], "uint16"),
+    "ys": ("sbuf", [128, 8], "float32"), "st4": ("sbuf", [128, 8], "float32"), "t4": ("sbuf", [128, 8], "float32"),
+    "rd": ("sbuf", [128, 8], "float32"), "GM": ("sbuf", [128, 512], "bfloat16"), "SB": ("sbuf", [128, 512], "bfloat16"),
+    "YU": ("sbuf", [128, 34], "uint16"), "Yd": ("sbuf", [128, 40], "float32"), "s1": ("sbuf", [128, 32], "float32"),
+    "s2": ("sbuf", [128, 32], "float32"), "s3": ("sbuf", [128, 32], "float32"), "s4": ("sbuf", [128, 32], "float32"),
+    "oU": ("sbuf", [128, 32], "uint16"), "inv": ("sbuf", [128, 1024], "bfloat16"), "NP": ("sbuf", [128, 24], "uint16"),
+    "sg": ("sbuf", [128, 400], "bfloat16"), "C0": ("sbuf", [128, 272], "bfloat16"), "C1": ("sbuf", [128, 272], "bfloat16"),
+    "SC": ("sbuf", [128, 272], "bfloat16"), "P1": ("sbuf", [128, 128], "bfloat16"), "P2": ("sbuf", [128, 64], "bfloat16"),
+    "P4": ("sbuf", [128, 32], "bfloat16"), "TU": ("sbuf", [128, 96], "uint16"), "Tr": ("sbuf", [128, 512], "bfloat16"),
+    "HL": ("sbuf", [128, 72], "uint16"), "yL": ("sbuf", [128, 96], "uint16"), "tL": ("sbuf", [128, 96], "uint16"),
+    "YR": ("sbuf", [128, 1536], "bfloat16"), "Z": ("sbuf", [128, 512], "bfloat16"), "MU": ("sbuf", [128, 72], "uint16"),
+    "mr": ("sbuf", [128, 384], "float32"),
+    "xq": ("sbuf", [128, 1536], "float8_e4m3fn_x4"), "xs": ("sbuf", [128, 1536], "uint8"), "hb": ("sbuf", [128, 1536], "bfloat16"),
+    "hq": ("sbuf", [128, 1152], "float8_e4m3fn_x4"), "hs": ("sbuf", [128, 1152], "uint8"),
+    "hL": ("sbuf", [128, 1152], "float8_e4m3fn_x4"), "hP": ("sbuf", [128, 1152], "uint8"),
+    "fb": ("sbuf", [128, 1536], "bfloat16"), "bb": ("sbuf", [128, 1536], "bfloat16"), "ab": ("sbuf", [128, 1536], "bfloat16"),
+    "xn": ("sbuf", [128, 1536], "bfloat16"), "yb": ("sbuf", [128, 384], "float32"),
+}
+for _k in range(8):
+    SCRATCH["ps%d" % _k] = ("psum", [128, 512], "float32")
+SEMAPHORES = (["cV", "cA", "cT", "cG", "loc"] + ["d%d" % k for k in range(24)] + ["ay%d" % k for k in range(3)]
+              + ["at%d" % k for k in range(3)] + ["ah%d_%d" % (r, k) for r in range(3) for k in range(len(CH))])
+
+
+def rank_program(g, core, T, topo):
+    rank = T.rank_of(core)
+    if rank is None:
+        return
+    op = AluOpType
+    eng = {"V": g.vector, "A": g.scalar, "T": g.tensor, "G": g, "Y": g.sync}
+    cnt = {q: 0 for q in eng}
+    know = {q: {} for q in eng}
+    snap = {}
+    acc = {}
+    dmas = []
+    loc = [0]
+
+    def R(n, a=0, b=None, s=1):
+        return (n, a, SCRATCH[n][1][1] if b is None else b, s)
+
+    def v(r):
+        n, a, b, s = r
+        return T[n][:, a:b] if s == 1 else T[n][:, a:b:s]
+
+    def meet(a, b):
+        if a[3] == b[3] and a[3] > 1 and (a[1] - b[1]) % a[3]:
+            return False
+        return a[1] < b[2] and b[1] < a[2]
+
+    def wait(q, tok):
+        if know[q].get(tok[0], 0) >= tok[1]:
+            return
+        eng[q].wait_ge(T.sem[tok[0]], tok[1])
+        for k, n in list(snap.get(tok, {}).items()) + [tok]:
+            know[q][k] = max(know[q].get(k, 0), n)
+
+    def order(q, rd, wr, dma=False):
+        need = {}
+        for r, w in [(r, False) for r in rd] + [(r, True) for r in wr]:
+            bank = r[0].startswith("ps")
+            for r0, w0, q0, tok in acc.get(r[0], []):
+                if bank:
+                    if q0 == q and not (w0 or w) or (q0 == q and q == "T"):
+                        continue
+                elif not (w or w0) or not meet(r, r0):
+                    continue
+                elif q0 == q and not w0 and tok[0] == "c" + q and not dma:
+                    continue
+                need[tok[0]] = max(need.get(tok[0], 0), tok[1])
+        for k in sorted(need):
+            wait(q, (k, need[k]))
+
+    def record(q, rd, wr, tok):
+        snap[tok] = dict(know[q])
+        for r, w in [(r, False) for r in rd] + [(r, True) for r in wr]:
+            l = acc.setdefault(r[0], [])
+            if w and r[3] == 1:
+                l[:] = [e for e in l if not (r[1] <= e[0][1] and e[0][2] <= r[2])]
+            if w and r[0].startswith("ps"):
+                l[:] = []
+            l.append((r, w, q, tok))
+
+    def emit(q, fn, rd, wr):
+        rd = [r for r in rd if isinstance(r, tuple)]
+        order(q, rd, wr)
+        cnt[q] += 1
+        fn().then_inc(T.sem["c" + q], 1)
+        record(q, rd, wr, ("c" + q, cnt[q]))
+
+    def dma(q, out, in_, rd, wr):
+        order(q, rd, wr, True)
+        s = "d%d" % len(dmas)
+        dmas.append((q, s))
+        eng[q].dma_start(out, in_).then_inc(T.sem[s], 16)
+        record(q, rd, wr, (s, 16))
+
+    def sc(x):
+        return v(x) if isinstance(x, tuple) else x
+
+    def tt(out, a, b, o, ind=None):
+        emit("V", lambda: g.vector.tensor_tensor(v(out), v(a).indirect(v(ind)) if ind else v(a), v(b), o), [a, b, ind], [out])
+
+    def ts(out, a, s1, s2, o1, o2=None):
+        if o2 is None:
+            emit("V", lambda: g.vector.tensor_scalar(v(out), v(a), sc(s1), None, o1), [a, s1], [out])
+        else:
+            emit("V", lambda: g.vector.tensor_scalar(v(out), v(a), sc(s1), sc(s2), o1, o2), [a, s1, s2], [out])
+
+    def tc(out, a, ind=None, oind=None):
+        emit("V", lambda: g.vector.tensor_copy(v(out).indirect(v(oind)) if oind else v(out), v(a).indirect(v(ind)) if ind else v(a)),
+             [a, ind, oind], [out])
+
+    def act(out, a, f=AF.Copy, ind=None, **k):
+        emit("A", lambda: g.scalar.activation(v(out), v(a).indirect(v(ind)) if ind else v(a), f, **k), [a, ind], [out])
+
+    def fill(out, x):
+        emit("V", lambda: g.vector.memset(v(out), x), [], [out])
+
+    def total(out, a):
+        emit("V", lambda: g.vector.tensor_reduce(v(out), v(a), AxisListType.X, op.add), [a], [out])
+
+    def scan(out, n, a):
+        emit("V", lambda: g.vector.tensor_tensor_scan(v(out), v(R("R0", 0, n)), v(a), 0.0, op.mult, op.add), [R("R0", 0, n), a], [out])
+
+    def quant(q, s, a):
+        emit("V", lambda: g.vector.quantize_mx(v(q), v(s), v(a)), [a], [q, s])
+
+    def mm(bank, n, lq, ls, rq, rs):
+        o = R("ps%d" % bank, 0, n)
+        emit("T", lambda: g.tensor.matmul_mx(v(o), v(lq), v(ls), v(rq), v(rs), True, True), [lq, ls, rq, rs], [o])
+
+    def iota(out, pat, base, cm=0):
+        kw = {} if SCRATCH[out[0]][2] == "int32" else {"allow_small_or_imprecise_dtypes": True}
+        emit("G", lambda: g.iota(v(out), pat, base, cm, **kw), [], [out])
+
+    def dist(win, ind, n):
+        tt(R("GM", 0, n), win, R("mk", 0, n), op.mult, ind)
+        scan(R("SB", 0, n), n, R("GM", 0, n))
+        return R("SB", 15, n, 16)
+
+    def b8(r):
+        return v(r).bitcast(dt.uint8)
+
+    dma("Y", v(R("seI")), T.se[:, :], [], [R("seI")])
+    dma("Y", v(R("ub")), T.u[:, :], [], [R("ub")])
+    for a, b in CH:
+        dma("Y", v(R("xb", 4 * a, 4 * b)), T.x[:, 4 * a:4 * b], [], [R("xb", 4 * a, 4 * b)])
+    dma("Y", b8(R("wq")), T.wc[:, :], [], [R("wq")])
+    dma("Y", v(R("wp")), T.ws[:, :], [], [R("wp")])
+    dma("Y", v(R("vb")), T.v[:, :], [], [R("vb")])
+    part = [T.cores[rank ^ s] for s in (1, 2, 3)]
+
+    def engs(a, b):
+        return topo.engines(a, b)
+
+    def some(e):
+        m = 0
+        for k in e:
+            m |= 1 << k
+        return m
+    cut = [(0, 4), (4, 6), (6, 8)]
+    for r in range(3):
+        n = len(engs(part[r], core))
+        acc.setdefault("yL", []).append((R("yL", 32 * r, 32 * r + 32), True, "R", ("ay%d" % r, cut[r][1] - cut[r][0])))
+        acc.setdefault("tL", []).append((R("tL", 32 * r, 32 * r + 32), True, "R", ("at%d" % r, n)))
+        for k, (a, b) in enumerate(CH):
+            for h in ("hL", "hP"):
+                acc.setdefault(h, []).append((R(h, C * r + a, C * r + b), True, "R", ("ah%d_%d" % (r, k), 2 * n)))
+
+    iota(R("KX"), [[0, 32]], 0, 1)
+    iota(R("iC", 0, 384), [[1, 384]], -256)
+    iota(R("tm"), [[0, 8], [1, 16]], 0, -1)
+    iota(R("ULi"), [[16, 8]], 0)
+    for a, n in ((0, 2), (2, 2), (4, 4), (8, 8)):
+        iota(R("rL", a, a + n), [[1, n]], 0 if a else -1)
+        iota(R("rA", a, a + n), [[0, n]], 256 // max(a, 1))
+        iota(R("rK", a, a + n), [[0, n]], 2 * max(a, 1))
+    for a, n, w in ((0, 2, 1), (2, 2, 4), (4, 1, 16)):
+        iota(R("rN", a, a + n), [[w, n]], w)
+    iota(R("iC", 384, 512), [[1, 128]], 128)
+    fill(R("hf"), 0.5)
+    fill(R("R0"), 1.0)
+    fill(R("R0", 0, 512, 16), 0.0)
+    fill(R("PS"), 0.0)
+    fill(R("TB", 0, 128), 15.0)
+    fill(R("TB", 128, 256), 16.0)
+    for a, b, m in ((0, 2, 0), (2, 4, 1), (4, 8, 3), (8, 16, 7), (16, 17, 15), (17, 18, 1)):
+        ts(R("KX", a, b), R("KX", a, b), m, None, op.bitwise_and)
+    for k in range(1, 4):
+        w = R("KX", 16 + 2 ** k, 16 + 2 ** (k + 1))
+        ts(w, w, k, 1, op.logical_shift_right, op.bitwise_and)
+    tc(R("KF"), R("KX"))
+    q_ = R("KF", 16, 17)
+
+    def bit(k):
+        return R("KF", 16 + 2 ** k, 17 + 2 ** k)
+    ts(R("AD", 0, 1), q_, 0.0, None, op.is_equal)
+    ts(R("tm"), R("tm"), 15, None, op.bitwise_and)
+    ts(R("mk", 0, 128), R("tm"), 0.0, None, op.is_equal)
+    tc(R("LT", 0, 1), bit(0))
+    act(R("Nc", 0, 768, 2), R("iC", 0, 384))
+    act(R("Nc", 1, 768, 2), R("iC", 0, 384))
+    act(R("AD", 1, 2), R("AD", 0, 1), AF.Identity, scale=768.0)
+    act(R("AD", 2, 3), R("AD", 0, 1), AF.Identity, scale=128.0, bias=256.0)
+    for k in range(1, 4):
+        act(R("AD", 2 + k, 3 + k), bit(k), AF.Identity, bias=512.0)
+    act(R("mk", 128, 256), R("mk", 0, 128))
+    act(R("mk", 256, 512), R("mk", 0, 256))
+    act(R("ys", 0, 1), q_, AF.Identity, scale=0.0, bias=-256.0)
+    act(R("H2", 0, 1), q_, AF.Identity, scale=0.0, bias=256.0)
+    act(R("H2", 1, 2), q_, AF.Identity, scale=0.0, bias=256.5)
+    act(R("sg", 384, 400), R("KF", 0, 16), AF.Identity, scale=0.0, bias=1.0)
+    act(R("Yd", 32, 40), R("KF", 0, 8), AF.Identity, scale=0.0, bias=1000.0)
+    act(R("bh"), R("KF", 16, 32), AF.Identity, bias=-0.5)
+    for m, n, w in ((0, 1, 8.0), (1, 2, 4.0), (3, 4, 2.0), (7, 8, 1.0)):
+        act(R("C0", 16 * m, 16 * (m + n)), R("mk", 16 * m, 16 * (m + n)), AF.Identity, scale=w)
+    tc(R("stU", 1, 24), R("seI", 1, 24))
+    ts(R("stU", 0, 1), R("seI", 0, 1), R("AD", 1, 2), None, op.add)
+    tc(R("Nc"), R("iC", 0, 384), oind=R("stU"))
+
+    def score(r, k):
+        a, b = CH[k]
+        bank = (0, 7)[k]
+        mm(bank, b - a, R("upq"), R("ups"), R("xq", C * r + a, C * r + b), R("xs", C * r + a, C * r + b))
+        act(R("sg", a, b), R("ps%d" % bank, 0, b - a), AF.Sign, bias=2.0 ** -93)
+
+    def pack_x(r, src):
+        for k, (a, b) in enumerate(CH):
+            quant(R("xq", C * r + a, C * r + b), R("xs", C * r + a, C * r + b), R(src, 4 * a, 4 * b))
+
+    HB = [[1, 2, 3, 4], [5, 6, 0, 7]]
+
+    def layer(r):
+        for k, (a, b) in enumerate(CH):
+            for t in range(4):
+                mm(HB[k][t], b - a, R("wq", 128 * t, 128 * t + 128), R("wp", 128 * t, 128 * t + 128),
+                   R("xq", C * r + a, C * r + b), R("xs", C * r + a, C * r + b))
+                act(R("hb", 4 * a + t, 4 * b, 4), R("ps%d" % HB[k][t], 0, b - a), scale=0.03125)
+
+    def pack_h(r, k):
+        a, b = CH[k]
+        quant(R("hq", C * r + a, C * r + b), R("hs", C * r + a, C * r + b), R("hb", 4 * a, 4 * b))
+
+    def remote(dst, out, in_, rd, sem):
+        order("G", rd, [], True)
+        rid, pid, _ = topo.addr(dst)
+        g.remote_dma(out_ap=out, in_ap=in_, remote_sem=T.sem[sem], local_sem=T.sem.loc, pid=pid, routing_id=rid,
+                     dma_engine_mask=topo.mask(core, dst))
+        loc[0] += len(engs(core, dst))
+
+    def send_h(r, k):
+        a, b = C * r + CH[k][0], C * r + CH[k][1]
+        remote(part[r], b8(R("hL", a, b)), b8(R("hq", a, b)), [R("hq", a, b)], "ah%d_%d" % (r, k))
+        remote(part[r], v(R("hP", a, b)), v(R("hs", a, b)), [R("hs", a, b)], "ah%d_%d" % (r, k))
+
+    def send_t(r):
+        w = (32 * r, 32 * r + 32)
+        remote(part[r], v(R("tL", *w)), v(R("TU", *w)), [R("TU", *w)], "at%d" % r)
+
+    def send_y():
+        order("G", [R("YU", 0, 32)], [], True)
+        tr = []
+        for r in range(3):
+            rid, pid, _ = topo.addr(part[r])
+            tr.append(RemoteDMATransfer(dst_ids=[DstId(rid=rid, pnc=pid)], remote_sem=T.sem["ay%d" % r], src=v(R("YU", 0, 32)),
+                                        dma_engine_mask=some(engs(core, part[r])[cut[r][0]:cut[r][1]]), dst=v(R("yL", 32 * r, 32 * r + 32))))
+            loc[0] += cut[r][1] - cut[r][0]
+        g.remote_dma_fused(tr, local_sem=T.sem.loc)
+
+    emit("G", lambda: g.affine_select(v(R("idn")), v(R("hf")), [[-1, 128]], op.is_equal, 0.0, 0, 1), [R("hf")], [R("idn")])
+    def table(n, o, items):
+        for a, pat, base in items:
+            m = 1
+            for _, c in pat:
+                m *= c
+            iota(R(n, o + a, o + a + m), pat, base)
+    one = [[0, 1]]
+    table("TB", 0, [(0, [[0, 2], [16, 8]], 127), (23, [[0, 2], [16, 4]], 63), (19, [[0, 2], [16, 2]], 31), (31, one, 271)])
+    table("TB", 32, [(0, [[0, 4], [16, 4]], 63), (23, [[0, 4], [16, 2]], 31)])
+    table("TB", 64, [(0, [[0, 8], [16, 2]], 31)])
+    up = [(0, [[0, 2], [1, 8]], 23), (23, [[0, 2], [1, 4]], 19), (19, [[0, 2], [1, 2]], 17)]
+    table("TB", 128, up)
+    table("TB", 160, [(0, [[0, 4], [1, 4]], 19), (23, [[0, 4], [1, 2]], 17)])
+    table("TB", 192, [(0, [[0, 8], [1, 2]], 17)])
+    table("TB", 224, up + [(16, one, 32), (31, one, 32)])
+    table("PS", 0, [(0, [[2, 2], [0, 8]], -1), (23, [[2, 2], [0, 4]], -1), (19, [[2, 2], [0, 2]], -1), (17, [[2, 2]], -1), (31, one, 1)])
+    table("PS", 32, [(0, [[0, 2], [2, 2], [0, 4]], -1), (23, [[0, 2], [2, 2], [0, 2]], -1), (19, [[0, 2], [2, 2]], -1)])
+    table("PS", 64, [(0, [[0, 4], [2, 2], [0, 2]], -1), (23, [[0, 4], [2, 2]], -1)])
+    table("PS", 96, [(0, [[0, 8], [2, 2]], -1)])
+    iota(R("JC"), [[16, 32]], 400, 1)
+    for b in range(4):
+        act(R("EB", 512 * b, 512 * b + 512), R("mk"), AF.Identity, scale=0.0)
+    for b in range(4):
+        act(R("EB", 512 * b + b, 512 * b + 512, 4), R("idn"))
+
+    lat, col = [0], [17, 19, 23, 0]
+
+    def level(l):
+        n = 2 << l
+        at = lat[0]
+        w = dist(R("Nc", 0, 768), R("LL", at, at + n), 16 * n)
+        if l < 3:
+            at += n
+            ts(R("LL", at, at + n), w, 2.0, 512.0, op.mult, op.add)
+            ts(R("LL", at + n, at + 2 * n), w, 2.0, 513.0, op.mult, op.add)
+            lat[0] = at
+        ts(R("YU", col[l], col[l] + n), w, 256.0, None, op.add)
+
+    for k in range(4):
+        tt(R("GM", 0, 16), R("Nc", 0, 768), R("mk", 0, 16), op.mult, R("LT", 2 * k, 2 * k + 1))
+        total(R("ys", k + 1, k + 2), R("GM", 0, 16))
+        if k < 3:
+            ts(R("LT", 2 * k + 2, 2 * k + 3), R("ys", k + 1, k + 2), 2.0, R("AD", k + 3, k + 4), op.mult, op.add)
+    ts(R("LL", 0, 2), R("H2"), R("ys", 4, 5), 2.0, op.add, op.mult)
+    ts(R("YU", 16, 17), R("ys", 4, 5), 256.0, None, op.add)
+    level(0)
+    tc(R("UL"), R("ULi"))
+    quant(R("uq"), R("us"), R("ub"))
+    emit("V", lambda: g.vector.tensor_copy(v(R("upq")).bitcast(dt.uint32), v(R("uq")).bitcast(dt.uint32).indirect(v(R("UL")))),
+         [R("uq"), R("UL")], [R("upq")])
+    act(R("ups"), R("us"), ind=R("UL"))
+    pack_x(0, "xb")
+    score(0, 0)
+    score(0, 1)
+    layer(0)
+    level(1)
+    ts(R("NK", 0, 5), R("rN", 0, 5), q_, -1.0, op.is_gt, op.mult)
+    tt(R("OH"), R("NK", 0, 4), R("NK", 1, 5), op.subtract)
+    tt(R("t4", 0, 4), R("OH"), R("ys", 0, 4), op.mult)
+    total(R("rd", 0, 1), R("t4", 0, 4))
+    for c in (31, 32):
+        ts(R("YU", c, c + 1), R("rd", 0, 1), R("AD", 2, 3), None, op.add)
+    level(2)
+    tt(R("eqm"), R("rL"), R("KF", 0, 16), op.is_equal)
+    tt(R("sx"), R("bh"), R("rA"), op.mult)
+    tt(R("C0", 240, 256), R("eqm"), R("sx"), op.mult)
+    ts(R("ow"), R("rK"), q_, -1.0, op.is_gt, op.mult)
+    tt(R("C0", 256, 272), R("C0", 240, 256), R("ow"), op.mult)
+    ts(R("C0", 256, 257), R("AD", 0, 1), -256.0, None, op.mult)
+    tt(R("TM"), R("TB"), R("mk", 0, 256), op.mult)
+    scan(R("TS"), 256, R("TM"))
+    tc(R("PL"), R("TS", 15, 256, 16))
+
+    def turned(r):
+        c0, c1 = ("C0", "C1") if r % 2 == 0 else ("C1", "C0")
+        tt(R(c1), R("sg"), R(c0), op.mult, R("YU", 16, 33))
+        scan(R("SC"), 272, R(c1))
+        tt(R("P1"), R("SC"), R("PS"), op.mult, R("PL", 0, 8))
+        tt(R("P2"), R("P1", 0, 64), R("P1", 64, 128), op.add)
+        tt(R("P4"), R("P2", 0, 32), R("P2", 32, 64), op.add)
+        ts(R("TU", 32 * r, 32 * r + 32), R("P4"), 256.0, R("SC", 255, 256), op.add, op.add)
+
+    def trep(r):
+        act(R("Tr"), R("iC"), ind=R("TU", 32 * r, 32 * r + 32))
+
+    def yrep(r):
+        act(R("YR", 512 * r, 512 * r + 512), R("iC"), ind=R("yL", 32 * r, 32 * r + 32))
+
+    def unpack(r, t):
+        mm(1 + t, C, R("eq", 128 * t, 128 * t + 128), R("es", 128 * t, 128 * t + 128), R("xq", C * r, C * r + C), R("xs", C * r, C * r + C))
+        if FQ[r][t] == "V":
+            tc(R("fb", C * t, C * t + C), R("ps%d" % (1 + t), 0, C))
+        else:
+            act(R("fb", C * t, C * t + C), R("ps%d" % (1 + t), 0, C))
+
+    def above(t):
+        act(R("bb", C * t, C * t + C), R("fb", C * t, C * t + C), ind=R("paU"))
+
+    def hlist(r):
+        w = dist(R("Tr"), R("NP"), C)
+        ts(R("HL", 24 * r, 24 * r + 24), w, 256.0, None, op.add)
+
+    def arrived(r):
+        for k, (a, b) in enumerate(CH):
+            for t in range(4):
+                bk = HB[1 - k][t]
+                mm(bk, b - a, R("eq", 128 * t, 128 * t + 128), R("es", 128 * t, 128 * t + 128),
+                   R("hL", C * r + a, C * r + b), R("hP", C * r + a, C * r + b))
+                act(R("ab", C * t + a, C * t + b), R("ps%d" % bk, 0, b - a))
+
+    def maps(r):
+        tc(R("Z"), R("YR", 512 * r, 512 * r + 512), oind=R("tL", 32 * r, 32 * r + 32))
+        w = dist(R("Z"), R("HL", 24 * r, 24 * r + 24), C)
+        ts(R("MU", 24 * r, 24 * r + 24), w, 256.0, None, op.add)
+
+    def renew(r):
+        for t in range(4):
+            tt(R("xn", t, 1536, 4), R("ab", C * t, C * t + C), R("bb", C * t, C * t + C), op.add, R("MU", 24 * r, 24 * r + 24))
+        pack_x(r + 1, "xn")
+
+    turned(0)
+    send_t(0)
+    level(3)
+    send_y()
+    for k in range(len(CH)):
+        pack_h(0, k)
+        send_h(0, k)
+    quant(R("eq"), R("es"), R("EB"))
+    trep(0)
+    yrep(0)
+    ts(R("paI"), R("seI"), 1, None, op.arith_shift_right)
+    tc(R("paU"), R("paI"))
+    for t in range(4):
+        unpack(0, t)
+    tc(R("Yd", 0, 32), R("YU", 0, 32))
+    tt(R("st4", 0, 4), R("ys", 0, 4), R("ys", 1, 5), op.is_equal)
+    total(R("rd", 1, 2), R("st4", 0, 4))
+    tt(R("t4", 4, 8), R("st4", 0, 4), R("NK", 1, 5), op.mult)
+    total(R("rd", 2, 3), R("t4", 4, 8))
+    tc(R("Ye"), R("YU", 0, 32))
+    tt(R("s1"), R("Yd"), R("Ye"), op.is_equal, R("PL", 14, 16))
+    tc(R("s5"), R("s1"), ind=R("PL", 8, 14))
+    tt(R("s2"), R("s5", 0, 32), R("s5", 32, 64), op.add)
+    tt(R("s4"), R("s5", 64, 96), R("s1"), op.add)
+    tt(R("s3"), R("s2"), R("s4"), op.add)
+    tt(R("s3", 31, 32), R("s3", 31, 32), R("rd", 2, 3), op.add)
+    ts(R("s4"), R("s3"), R("rd", 1, 2), 1.0, op.add, op.min)
+    tt(R("s2"), R("JC"), R("s4"), op.mult)
+    tt(R("s1"), R("s2"), R("Yd", 0, 32), op.max)
+    tc(R("oU"), R("s1"))
+    tc(R("inv"), R("iC"), oind=R("oU"))
+    tt(R("GM", 0, C), R("inv", 0, C), R("mk", 0, C), op.mult)
+    scan(R("SB", 0, C), C, R("GM", 0, C))
+    ts(R("NP"), R("SB", 15, C, 16), 256.0, None, op.add)
+    hlist(0)
+    for t in range(4):
+        above(t)
+    arrived(0)
+    maps(0)
+    renew(0)
+    for r in (1, 2):
+        score(r, 0)
+        score(r, 1)
+        layer(r)
+        turned(r)
+        send_t(r)
+        for k in range(len(CH)):
+            pack_h(r, k)
+            send_h(r, k)
+        if r == 1:
+            quant(R("vq"), R("vs"), R("vb"))
+        trep(r)
+        if r == 1:
+            yrep(1)
+            yrep(2)
+        for t in range(4):
+            if t == 2:
+                hlist(r)
+            unpack(r, t)
+        for t in range(4):
+            above(t)
+        arrived(r)
+        maps(r)
+        if r == 2:
+            act(R("mr"), R("Z"), AF.Identity, ind=R("HL", 48, 72), bias=256.0)
+            dma("Y", T.im[:, :], T.mr[0:128:16, 0:C], [R("mr")], [])
+        renew(r)
+    for k, (a, b) in enumerate(CH):
+        q3, s3 = R("xq", 3 * C + a, 3 * C + b), R("xs", 3 * C + a, 3 * C + b)
+        mm((0, 7)[k], b - a, R("vq"), R("vs"), q3, s3)
+        act(R("yb", a, b), R("ps%d" % (0, 7)[k], 0, b - a))
+        dma("Y", T.oc[:, 4 * a:4 * b], b8(q3), [q3], [])
+        dma("A", T.y[:, a:b], v(R("yb", a, b)), [R("yb", a, b)], [])
+    for k in range(4):
+        dma("Y", T.osc[4 * k:4 * k + 4, :], T.xs[32 * k:32 * k + 4, 3 * C:4 * C], [R("xs", 3 * C, 4 * C)], [])
+    for q, s in dmas:
+        wait(q, (s, 16))
+    for q in ("V", "A", "T", "G"):
+        g.wait_ge(T.sem["c" + q], cnt[q])
+    g.wait_ge(T.sem.loc, loc[0])

@@ -3,7 +3,8 @@ from concourse.mybir import dt, AluOpType, AxisListType, ActivationFunctionType 
 
 C = 384
 CH = [(0, 192), (192, 384)]
-FQ = ["AAAA", "VVVA", "VVVA"]
+HC = [(0, 128), (128, 384)]
+FQ = ["AAAA", "AVVV", "AVVV"]
 SCRATCH = {
     "KX": ("sbuf", [128, 32], "int32"), "KF": ("sbuf", [128, 32], "float32"), "tm": ("sbuf", [128, 128], "int32"),
     "AD": ("sbuf", [128, 8], "float32"), "rL": ("sbuf", [128, 16], "float32"), "rA": ("sbuf", [128, 16], "float32"),
@@ -11,14 +12,18 @@ SCRATCH = {
     "eqm": ("sbuf", [128, 16], "float32"), "sx": ("sbuf", [128, 16], "float32"), "ow": ("sbuf", [128, 16], "float32"),
     "NK": ("sbuf", [128, 8], "float32"), "OH": ("sbuf", [128, 4], "float32"), "H2": ("sbuf", [128, 2], "float32"),
     "iC": ("sbuf", [128, 512], "bfloat16"), "mk": ("sbuf", [128, 512], "bfloat16"), "R0": ("sbuf", [128, 512], "bfloat16"),
-    "TB": ("sbuf", [128, 256], "float32"), "TM": ("sbuf", [128, 256], "float32"), "TS": ("sbuf", [128, 256], "float32"),
-    "PL": ("sbuf", [128, 16], "uint16"), "PS": ("sbuf", [128, 128], "bfloat16"), "Ye": ("sbuf", [128, 32], "float32"),
-    "s5": ("sbuf", [128, 96], "float32"), "ULi": ("sbuf", [128, 8], "int32"),
+    "TB": ("sbuf", [128, 288], "float32"), "MX": ("sbuf", [128, 384], "bfloat16"), "SF": ("sbuf", [128, 384], "float32"),
+    "R4": ("sbuf", [128, 128], "bfloat16"), "GA": ("sbuf", [128, 384], "bfloat16"), "SB2": ("sbuf", [128, 224], "bfloat16"),
+    "PL": ("sbuf", [128, 18], "uint16"), "PS": ("sbuf", [128, 128], "bfloat16"), "Ye": ("sbuf", [128, 32], "float32"),
+    "s5": ("sbuf", [128, 128], "float32"), "s6": ("sbuf", [128, 128], "float32"),
+    "ULi": ("sbuf", [128, 8], "int32"),
     "UL": ("sbuf", [128, 8], "uint16"), "JC": ("sbuf", [128, 32], "float32"), "hf": ("sbuf", [128, 128], "bfloat16"),
     "idn": ("sbuf", [128, 128], "bfloat16"), "EB": ("sbuf", [128, 2048], "bfloat16"),
     "eq": ("sbuf", [128, 512], "float8_e4m3fn_x4"), "es": ("sbuf", [128, 512], "uint8"),
     "seI": ("sbuf", [128, 24], "int32"), "paI": ("sbuf", [128, 24], "int32"), "paU": ("sbuf", [128, 24], "uint16"),
-    "stU": ("sbuf", [128, 24], "uint16"), "xb": ("sbuf", [128, 1536], "bfloat16"), "ub": ("sbuf", [128, 512], "bfloat16"),
+    "slI": ("sbuf", [128, 24], "int32"), "sh": ("sbuf", [128, 24], "float32"), "sb": ("sbuf", [128, 24], "float32"),
+    "sw": ("sbuf", [128, 24], "float32"), "s24": ("sbuf", [128, 24], "float32"), "stU": ("sbuf", [128, 24], "uint16"),
+    "xb": ("sbuf", [128, 1536], "bfloat16"), "ub": ("sbuf", [128, 512], "bfloat16"),
     "vb": ("sbuf", [128, 512], "bfloat16"), "wq": ("sbuf", [128, 512], "float8_e4m3fn_x4"), "wp": ("sbuf", [128, 512], "uint8"),
     "uq": ("sbuf", [128, 128], "float8_e4m3fn_x4"), "us": ("sbuf", [128, 128], "uint8"),
     "upq": ("sbuf", [128, 128], "float8_e4m3fn_x4"), "ups": ("sbuf", [128, 128], "uint8"),
@@ -30,8 +35,8 @@ SCRATCH = {
     "s2": ("sbuf", [128, 32], "float32"), "s3": ("sbuf", [128, 32], "float32"), "s4": ("sbuf", [128, 32], "float32"),
     "oU": ("sbuf", [128, 32], "uint16"), "inv": ("sbuf", [128, 1024], "bfloat16"), "NP": ("sbuf", [128, 24], "uint16"),
     "sg": ("sbuf", [128, 400], "bfloat16"), "C0": ("sbuf", [128, 272], "bfloat16"), "C1": ("sbuf", [128, 272], "bfloat16"),
-    "SC": ("sbuf", [128, 272], "bfloat16"), "P1": ("sbuf", [128, 128], "bfloat16"), "P2": ("sbuf", [128, 64], "bfloat16"),
-    "P4": ("sbuf", [128, 32], "bfloat16"), "TU": ("sbuf", [128, 96], "uint16"), "Tr": ("sbuf", [128, 512], "bfloat16"),
+    "SC": ("sbuf", [128, 272], "bfloat16"), "P1": ("sbuf", [128, 128], "bfloat16"), "P4": ("sbuf", [128, 128], "bfloat16"),
+    "TU": ("sbuf", [128, 96], "uint16"), "Tr": ("sbuf", [128, 512], "bfloat16"),
     "HL": ("sbuf", [128, 72], "uint16"), "yL": ("sbuf", [128, 96], "uint16"), "tL": ("sbuf", [128, 96], "uint16"),
     "YR": ("sbuf", [128, 1536], "bfloat16"), "Z": ("sbuf", [128, 512], "bfloat16"), "MU": ("sbuf", [128, 72], "uint16"),
     "mr": ("sbuf", [128, 384], "float32"),
@@ -44,7 +49,8 @@ SCRATCH = {
 for _k in range(8):
     SCRATCH["ps%d" % _k] = ("psum", [128, 512], "float32")
 SEMAPHORES = (["cV", "cA", "cT", "cG", "loc"] + ["d%d" % k for k in range(24)] + ["ay%d" % k for k in range(3)]
-              + ["at%d" % k for k in range(3)] + ["ah%d_%d" % (r, k) for r in range(3) for k in range(len(CH))])
+              + ["at%d" % k for k in range(3)] + ["as%d" % k for k in range(3)]
+              + ["ah%d_%d" % (r, k) for r in range(3) for k in range(len(HC))])
 
 
 def rank_program(g, core, T, topo):
@@ -88,8 +94,6 @@ def rank_program(g, core, T, topo):
                     if q0 == q and not (w0 or w) or (q0 == q and q == "T"):
                         continue
                 elif not (w or w0) or not meet(r, r0):
-                    continue
-                elif q0 == q and not w0 and tok[0] == "c" + q and not dma:
                     continue
                 need[tok[0]] = max(need.get(tok[0], 0), tok[1])
         for k in sorted(need):
@@ -144,8 +148,13 @@ def rank_program(g, core, T, topo):
     def total(out, a):
         emit("V", lambda: g.vector.tensor_reduce(v(out), v(a), AxisListType.X, op.add), [a], [out])
 
-    def scan(out, n, a):
-        emit("V", lambda: g.vector.tensor_tensor_scan(v(out), v(R("R0", 0, n)), v(a), 0.0, op.mult, op.add), [R("R0", 0, n), a], [out])
+    def scan(out, n, a, z="R0"):
+        emit("V", lambda: g.vector.tensor_tensor_scan(v(out), v(R(z, 0, n)), v(a), 0.0, op.mult, op.add), [R(z, 0, n), a], [out])
+
+    def hold(out, n, a):
+        f = R("SF", 0, n)
+        emit("V", lambda: g.vector.tensor_tensor_scan(v(f), v(R("MX", 0, n)), v(a), 0.0, op.add, op.max), [R("MX", 0, n), a], [f])
+        ts(out, R("SF", 15, n, 16), R("AD", 6, 7), None, op.add)
 
     def quant(q, s, a):
         emit("V", lambda: g.vector.quantize_mx(v(q), v(s), v(a)), [a], [q, s])
@@ -158,10 +167,18 @@ def rank_program(g, core, T, topo):
         kw = {} if SCRATCH[out[0]][2] == "int32" else {"allow_small_or_imprecise_dtypes": True}
         emit("G", lambda: g.iota(v(out), pat, base, cm, **kw), [], [out])
 
-    def dist(win, ind, n):
+    rest = []
+
+    def slip():
+        if rest:
+            rest.pop(0)()
+
+    def dist(win, ind, n, o="SB", a=0):
         tt(R("GM", 0, n), win, R("mk", 0, n), op.mult, ind)
-        scan(R("SB", 0, n), n, R("GM", 0, n))
-        return R("SB", 15, n, 16)
+        slip()
+        scan(R(o, a, a + n), n, R("GM", 0, n))
+        slip()
+        return R(o, a + 15, a + n, 16)
 
     def b8(r):
         return v(r).bitcast(dt.uint8)
@@ -188,9 +205,9 @@ def rank_program(g, core, T, topo):
         n = len(engs(part[r], core))
         acc.setdefault("yL", []).append((R("yL", 32 * r, 32 * r + 32), True, "R", ("ay%d" % r, cut[r][1] - cut[r][0])))
         acc.setdefault("tL", []).append((R("tL", 32 * r, 32 * r + 32), True, "R", ("at%d" % r, n)))
-        for k, (a, b) in enumerate(CH):
-            for h in ("hL", "hP"):
-                acc.setdefault(h, []).append((R(h, C * r + a, C * r + b), True, "R", ("ah%d_%d" % (r, k), 2 * n)))
+        acc.setdefault("hP", []).append((R("hP", C * r, C * r + C), True, "R", ("as%d" % r, n)))
+        for k, (a, b) in enumerate(HC):
+            acc.setdefault("hL", []).append((R("hL", C * r + a, C * r + b), True, "R", ("ah%d_%d" % (r, k), n)))
 
     iota(R("KX"), [[0, 32]], 0, 1)
     iota(R("iC", 0, 384), [[1, 384]], -256)
@@ -207,8 +224,10 @@ def rank_program(g, core, T, topo):
     fill(R("R0"), 1.0)
     fill(R("R0", 0, 512, 16), 0.0)
     fill(R("PS"), 0.0)
-    fill(R("TB", 0, 128), 15.0)
-    fill(R("TB", 128, 256), 16.0)
+    fill(R("TB", 0, 128), -241.0)
+    fill(R("TB", 128, 288), -240.0)
+    fill(R("R4"), 1.0)
+    fill(R("R4", 0, 128, 4), 0.0)
     for a, b, m in ((0, 2, 0), (2, 4, 1), (4, 8, 3), (8, 16, 7), (16, 17, 15), (17, 18, 1)):
         ts(R("KX", a, b), R("KX", a, b), m, None, op.bitwise_and)
     for k in range(1, 4):
@@ -231,6 +250,8 @@ def rank_program(g, core, T, topo):
         act(R("AD", 2 + k, 3 + k), bit(k), AF.Identity, bias=512.0)
     act(R("mk", 128, 256), R("mk", 0, 128))
     act(R("mk", 256, 512), R("mk", 0, 256))
+    act(R("AD", 6, 7), q_, AF.Identity, scale=512.0, bias=-7424.0)
+    act(R("MX"), R("mk", 0, 384), AF.Identity, scale=-33280.0, bias=512.0)
     act(R("ys", 0, 1), q_, AF.Identity, scale=0.0, bias=-256.0)
     act(R("H2", 0, 1), q_, AF.Identity, scale=0.0, bias=256.0)
     act(R("H2", 1, 2), q_, AF.Identity, scale=0.0, bias=256.5)
@@ -239,9 +260,13 @@ def rank_program(g, core, T, topo):
     act(R("bh"), R("KF", 16, 32), AF.Identity, bias=-0.5)
     for m, n, w in ((0, 1, 8.0), (1, 2, 4.0), (3, 4, 2.0), (7, 8, 1.0)):
         act(R("C0", 16 * m, 16 * (m + n)), R("mk", 16 * m, 16 * (m + n)), AF.Identity, scale=w)
-    tc(R("stU", 1, 24), R("seI", 1, 24))
-    ts(R("stU", 0, 1), R("seI", 0, 1), R("AD", 1, 2), None, op.add)
-    tc(R("Nc"), R("iC", 0, 384), oind=R("stU"))
+    ts(R("paI"), R("seI"), 1, None, op.arith_shift_right)
+    ts(R("slI"), R("seI"), 1, None, op.bitwise_and)
+    tc(R("paU"), R("paI"))
+    ts(R("sh"), R("slI"), -1.0, 0.5, op.mult, op.add)
+    tt(R("sb"), R("seI"), R("sh"), op.add)
+    ts(R("sb", 0, 1), R("sb", 0, 1), R("AD", 1, 2), None, op.add)
+    fill(R("EB"), 0.0)
 
     def score(r, k):
         a, b = CH[k]
@@ -256,14 +281,14 @@ def rank_program(g, core, T, topo):
     HB = [[1, 2, 3, 4], [5, 6, 0, 7]]
 
     def layer(r):
-        for k, (a, b) in enumerate(CH):
+        for k, (a, b) in enumerate(HC):
             for t in range(4):
                 mm(HB[k][t], b - a, R("wq", 128 * t, 128 * t + 128), R("wp", 128 * t, 128 * t + 128),
                    R("xq", C * r + a, C * r + b), R("xs", C * r + a, C * r + b))
                 act(R("hb", 4 * a + t, 4 * b, 4), R("ps%d" % HB[k][t], 0, b - a), scale=0.03125)
 
     def pack_h(r, k):
-        a, b = CH[k]
+        a, b = HC[k]
         quant(R("hq", C * r + a, C * r + b), R("hs", C * r + a, C * r + b), R("hb", 4 * a, 4 * b))
 
     def remote(dst, out, in_, rd, sem):
@@ -274,9 +299,12 @@ def rank_program(g, core, T, topo):
         loc[0] += len(engs(core, dst))
 
     def send_h(r, k):
-        a, b = C * r + CH[k][0], C * r + CH[k][1]
+        a, b = C * r + HC[k][0], C * r + HC[k][1]
         remote(part[r], b8(R("hL", a, b)), b8(R("hq", a, b)), [R("hq", a, b)], "ah%d_%d" % (r, k))
-        remote(part[r], v(R("hP", a, b)), v(R("hs", a, b)), [R("hs", a, b)], "ah%d_%d" % (r, k))
+
+    def send_s(r):
+        w = (C * r, C * r + C)
+        remote(part[r], v(R("hP", *w)), v(R("hs", *w)), [R("hs", *w)], "as%d" % r)
 
     def send_t(r):
         w = (32 * r, 32 * r + 32)
@@ -293,90 +321,29 @@ def rank_program(g, core, T, topo):
         g.remote_dma_fused(tr, local_sem=T.sem.loc)
 
     emit("G", lambda: g.affine_select(v(R("idn")), v(R("hf")), [[-1, 128]], op.is_equal, 0.0, 0, 1), [R("hf")], [R("idn")])
-    def table(n, o, items):
+    def table(n, o, s, items):
         for a, pat, base in items:
             m = 1
             for _, c in pat:
                 m *= c
-            iota(R(n, o + a, o + a + m), pat, base)
+            iota(R(n, o + s * a, o + s * (a + m - 1) + 1, s), pat, base - 256 if n == "TB" else base)
     one = [[0, 1]]
-    table("TB", 0, [(0, [[0, 2], [16, 8]], 127), (23, [[0, 2], [16, 4]], 63), (19, [[0, 2], [16, 2]], 31), (31, one, 271)])
-    table("TB", 32, [(0, [[0, 4], [16, 4]], 63), (23, [[0, 4], [16, 2]], 31)])
-    table("TB", 64, [(0, [[0, 8], [16, 2]], 31)])
+    table("TB", 0, 4, [(0, [[0, 2], [16, 8]], 127), (23, [[0, 2], [16, 4]], 63), (19, [[0, 2], [16, 2]], 31), (31, one, 271)])
+    table("TB", 1, 4, [(0, [[0, 4], [16, 4]], 63), (23, [[0, 4], [16, 2]], 31)])
+    table("TB", 2, 4, [(0, [[0, 8], [16, 2]], 31)])
     up = [(0, [[0, 2], [1, 8]], 23), (23, [[0, 2], [1, 4]], 19), (19, [[0, 2], [1, 2]], 17)]
-    table("TB", 128, up)
-    table("TB", 160, [(0, [[0, 4], [1, 4]], 19), (23, [[0, 4], [1, 2]], 17)])
-    table("TB", 192, [(0, [[0, 8], [1, 2]], 17)])
-    table("TB", 224, up + [(16, one, 32), (31, one, 32)])
-    table("PS", 0, [(0, [[2, 2], [0, 8]], -1), (23, [[2, 2], [0, 4]], -1), (19, [[2, 2], [0, 2]], -1), (17, [[2, 2]], -1), (31, one, 1)])
-    table("PS", 32, [(0, [[0, 2], [2, 2], [0, 4]], -1), (23, [[0, 2], [2, 2], [0, 2]], -1), (19, [[0, 2], [2, 2]], -1)])
-    table("PS", 64, [(0, [[0, 4], [2, 2], [0, 2]], -1), (23, [[0, 4], [2, 2]], -1)])
-    table("PS", 96, [(0, [[0, 8], [2, 2]], -1)])
+    table("PS", 0, 4, [(0, [[2, 2], [0, 8]], -1), (23, [[2, 2], [0, 4]], -1), (19, [[2, 2], [0, 2]], -1), (17, [[2, 2]], -1), (31, one, 1)])
+    table("PS", 1, 4, [(0, [[0, 2], [2, 2], [0, 4]], -1), (23, [[0, 2], [2, 2], [0, 2]], -1), (19, [[0, 2], [2, 2]], -1)])
+    table("PS", 2, 4, [(0, [[0, 4], [2, 2], [0, 2]], -1), (23, [[0, 4], [2, 2]], -1)])
+    table("PS", 3, 4, [(0, [[0, 8], [2, 2]], -1)])
+    table("TB", 128, 4, [(0, [[1, 32]], 0)])
+    table("TB", 129, 4, up)
+    table("TB", 130, 4, [(0, [[0, 4], [1, 4]], 19), (23, [[0, 4], [1, 2]], 17)])
+    table("TB", 131, 4, [(0, [[0, 8], [1, 2]], 17)])
+    table("TB", 256, 1, up + [(16, one, 32), (31, one, 32)])
     iota(R("JC"), [[16, 32]], 400, 1)
     for b in range(4):
-        act(R("EB", 512 * b, 512 * b + 512), R("mk"), AF.Identity, scale=0.0)
-    for b in range(4):
         act(R("EB", 512 * b + b, 512 * b + 512, 4), R("idn"))
-
-    lat, col = [0], [17, 19, 23, 0]
-
-    def level(l):
-        n = 2 << l
-        at = lat[0]
-        w = dist(R("Nc", 0, 768), R("LL", at, at + n), 16 * n)
-        if l < 3:
-            at += n
-            ts(R("LL", at, at + n), w, 2.0, 512.0, op.mult, op.add)
-            ts(R("LL", at + n, at + 2 * n), w, 2.0, 513.0, op.mult, op.add)
-            lat[0] = at
-        ts(R("YU", col[l], col[l] + n), w, 256.0, None, op.add)
-
-    for k in range(4):
-        tt(R("GM", 0, 16), R("Nc", 0, 768), R("mk", 0, 16), op.mult, R("LT", 2 * k, 2 * k + 1))
-        total(R("ys", k + 1, k + 2), R("GM", 0, 16))
-        if k < 3:
-            ts(R("LT", 2 * k + 2, 2 * k + 3), R("ys", k + 1, k + 2), 2.0, R("AD", k + 3, k + 4), op.mult, op.add)
-    ts(R("LL", 0, 2), R("H2"), R("ys", 4, 5), 2.0, op.add, op.mult)
-    ts(R("YU", 16, 17), R("ys", 4, 5), 256.0, None, op.add)
-    level(0)
-    tc(R("UL"), R("ULi"))
-    quant(R("uq"), R("us"), R("ub"))
-    emit("V", lambda: g.vector.tensor_copy(v(R("upq")).bitcast(dt.uint32), v(R("uq")).bitcast(dt.uint32).indirect(v(R("UL")))),
-         [R("uq"), R("UL")], [R("upq")])
-    act(R("ups"), R("us"), ind=R("UL"))
-    pack_x(0, "xb")
-    score(0, 0)
-    score(0, 1)
-    layer(0)
-    level(1)
-    ts(R("NK", 0, 5), R("rN", 0, 5), q_, -1.0, op.is_gt, op.mult)
-    tt(R("OH"), R("NK", 0, 4), R("NK", 1, 5), op.subtract)
-    tt(R("t4", 0, 4), R("OH"), R("ys", 0, 4), op.mult)
-    total(R("rd", 0, 1), R("t4", 0, 4))
-    for c in (31, 32):
-        ts(R("YU", c, c + 1), R("rd", 0, 1), R("AD", 2, 3), None, op.add)
-    level(2)
-    tt(R("eqm"), R("rL"), R("KF", 0, 16), op.is_equal)
-    tt(R("sx"), R("bh"), R("rA"), op.mult)
-    tt(R("C0", 240, 256), R("eqm"), R("sx"), op.mult)
-    ts(R("ow"), R("rK"), q_, -1.0, op.is_gt, op.mult)
-    tt(R("C0", 256, 272), R("C0", 240, 256), R("ow"), op.mult)
-    ts(R("C0", 256, 257), R("AD", 0, 1), -256.0, None, op.mult)
-    tt(R("TM"), R("TB"), R("mk", 0, 256), op.mult)
-    scan(R("TS"), 256, R("TM"))
-    tc(R("PL"), R("TS", 15, 256, 16))
-
-    def turned(r):
-        c0, c1 = ("C0", "C1") if r % 2 == 0 else ("C1", "C0")
-        tt(R(c1), R("sg"), R(c0), op.mult, R("YU", 16, 33))
-        scan(R("SC"), 272, R(c1))
-        tt(R("P1"), R("SC"), R("PS"), op.mult, R("PL", 0, 8))
-        tt(R("P2"), R("P1", 0, 64), R("P1", 64, 128), op.add)
-        tt(R("P4"), R("P2", 0, 32), R("P2", 32, 64), op.add)
-        ts(R("TU", 32 * r, 32 * r + 32), R("P4"), 256.0, R("SC", 255, 256), op.add, op.add)
-
-    def trep(r):
-        act(R("Tr"), R("iC"), ind=R("TU", 32 * r, 32 * r + 32))
 
     def yrep(r):
         act(R("YR", 512 * r, 512 * r + 512), R("iC"), ind=R("yL", 32 * r, 32 * r + 32))
@@ -391,12 +358,103 @@ def rank_program(g, core, T, topo):
     def above(t):
         act(R("bb", C * t, C * t + C), R("fb", C * t, C * t + C), ind=R("paU"))
 
+    def level(l):
+        n, at, o = 2 << l, (2 << l) - 2, 16 * ((2 << l) - 2)
+        w = dist(R("Nc", 0, 768), R("LL", at, at + n), 16 * n, "SB2", o)
+        at += n
+        ts(R("LL", at, at + n), w, 2.0, 512.0, op.mult, op.add)
+        ts(R("LL", at + n, at + 2 * n), w, 2.0, 513.0, op.mult, op.add)
+
+    tc(R("UL"), R("ULi"))
+    ts(R("NK", 0, 5), R("rN", 0, 5), q_, -1.0, op.is_gt, op.mult)
+    tt(R("eqm"), R("rL"), R("KF", 0, 16), op.is_equal)
+    tt(R("OH"), R("NK", 0, 4), R("NK", 1, 5), op.subtract)
+    quant(R("uq"), R("us"), R("ub"))
+    act(R("ups"), R("us"), ind=R("UL"))
+    emit("V", lambda: g.vector.tensor_copy(v(R("upq")).bitcast(dt.uint32), v(R("uq")).bitcast(dt.uint32).indirect(v(R("UL")))),
+         [R("uq"), R("UL")], [R("upq")])
+    tt(R("sx"), R("bh"), R("rA"), op.mult)
+    ts(R("ow"), R("rK"), q_, -1.0, op.is_gt, op.mult)
+    tt(R("C0", 240, 256), R("eqm"), R("sx"), op.mult)
+    pack_x(0, "xb")
+    score(0, 0)
+    score(0, 1)
+    quant(R("eq"), R("es"), R("EB"))
+    tt(R("C0", 256, 272), R("C0", 240, 256), R("ow"), op.mult)
+    ts(R("C0", 256, 257), R("AD", 0, 1), -256.0, None, op.mult)
+    for t in range(4):
+        unpack(0, t)
+    layer(0)
+    for t in range(4):
+        above(t)
+    w = dist(R("sg", 0, 400), R("paU"), C)
+    tt(R("sw"), w, R("sh"), op.mult)
+    tt(R("s24"), R("sb"), R("sw"), op.subtract)
+    tc(R("stU"), R("s24"))
+    tc(R("Nc"), R("iC", 0, 384), oind=R("stU"))
+    for k in range(4):
+        tt(R("GM", 0, 16), R("Nc", 0, 768), R("mk", 0, 16), op.mult, R("LT", 2 * k, 2 * k + 1))
+        slip()
+        total(R("ys", k + 1, k + 2), R("GM", 0, 16))
+        slip()
+        if k < 3:
+            ts(R("LT", 2 * k + 2, 2 * k + 3), R("ys", k + 1, k + 2), 2.0, R("AD", k + 3, k + 4), op.mult, op.add)
+        if k == 1:
+            pack_h(0, 0)
+            pack_h(0, 1)
+            send_h(0, 0)
+            send_s(0)
+            send_h(0, 1)
+    ts(R("LL", 0, 2), R("H2"), R("ys", 4, 5), 2.0, op.add, op.mult)
+    rest.extend([
+        lambda: tt(R("t4", 0, 4), R("OH"), R("ys", 0, 4), op.mult),
+        lambda: ts(R("YU", 16, 17), R("ys", 4, 5), 256.0, None, op.add),
+    ])
+    slip()
+    level(0)
+    rest.extend([
+        lambda: total(R("rd", 0, 1), R("t4", 0, 4)),
+        lambda: tt(R("st4", 0, 4), R("ys", 0, 4), R("ys", 1, 5), op.is_equal),
+        lambda: ts(R("YU", 31, 32), R("rd", 0, 1), R("AD", 2, 3), None, op.add),
+        lambda: total(R("rd", 1, 2), R("st4", 0, 4)),
+        lambda: tt(R("t4", 4, 8), R("st4", 0, 4), R("NK", 1, 5), op.mult),
+        lambda: ts(R("YU", 32, 33), R("rd", 0, 1), R("AD", 2, 3), None, op.add),
+        lambda: total(R("rd", 2, 3), R("t4", 4, 8)),
+    ])
+    level(1)
+    level(2)
+    act(R("GA", 0, 256), R("Nc", 0, 768), ind=R("LL", 14, 30))
+    ts(R("YU", 17, 31), R("SB2", 15, 224, 16), 256.0, None, op.add)
+    while rest:
+        slip()
+    hold(R("YU", 0, 16), 256, R("GA", 0, 256))
+    send_y()
+    hold(R("PL"), 288, R("TB"))
+    yrep(0)
+
+    def turned(r):
+        c0, c1 = ("C0", "C1") if r == 1 else ("C1", "C0")
+        tt(R(c1), R("sg"), R(c0), op.mult, R("YU", 16, 33))
+        scan(R("SC"), 272, R(c1))
+        pack_h(r, 0)
+        tt(R("P1"), R("SC"), R("PS"), op.mult, R("PL", 0, 8))
+        scan(R("P4"), 128, R("P1"), "R4")
+        ts(R("TU", 32 * r, 32 * r + 32), R("P4", 3, 128, 4), 256.0, R("SC", 255, 256), op.add, op.add)
+        pack_h(r, 1)
+        send_h(r, 0)
+        send_t(r)
+        send_s(r)
+        send_h(r, 1)
+
+    def trep(r):
+        act(R("Tr"), R("iC"), ind=R("TU", 32 * r, 32 * r + 32))
+
     def hlist(r):
         w = dist(R("Tr"), R("NP"), C)
         ts(R("HL", 24 * r, 24 * r + 24), w, 256.0, None, op.add)
 
     def arrived(r):
-        for k, (a, b) in enumerate(CH):
+        for k, (a, b) in enumerate(HC):
             for t in range(4):
                 bk = HB[1 - k][t]
                 mm(bk, b - a, R("eq", 128 * t, 128 * t + 128), R("es", 128 * t, 128 * t + 128),
@@ -413,63 +471,35 @@ def rank_program(g, core, T, topo):
             tt(R("xn", t, 1536, 4), R("ab", C * t, C * t + C), R("bb", C * t, C * t + C), op.add, R("MU", 24 * r, 24 * r + 24))
         pack_x(r + 1, "xn")
 
-    turned(0)
-    send_t(0)
-    level(3)
-    send_y()
-    for k in range(len(CH)):
-        pack_h(0, k)
-        send_h(0, k)
-    quant(R("eq"), R("es"), R("EB"))
-    trep(0)
-    yrep(0)
-    ts(R("paI"), R("seI"), 1, None, op.arith_shift_right)
-    tc(R("paU"), R("paI"))
-    for t in range(4):
-        unpack(0, t)
+
     tc(R("Yd", 0, 32), R("YU", 0, 32))
-    tt(R("st4", 0, 4), R("ys", 0, 4), R("ys", 1, 5), op.is_equal)
-    total(R("rd", 1, 2), R("st4", 0, 4))
-    tt(R("t4", 4, 8), R("st4", 0, 4), R("NK", 1, 5), op.mult)
-    total(R("rd", 2, 3), R("t4", 4, 8))
     tc(R("Ye"), R("YU", 0, 32))
-    tt(R("s1"), R("Yd"), R("Ye"), op.is_equal, R("PL", 14, 16))
-    tc(R("s5"), R("s1"), ind=R("PL", 8, 14))
-    tt(R("s2"), R("s5", 0, 32), R("s5", 32, 64), op.add)
-    tt(R("s4"), R("s5", 64, 96), R("s1"), op.add)
-    tt(R("s3"), R("s2"), R("s4"), op.add)
-    tt(R("s3", 31, 32), R("s3", 31, 32), R("rd", 2, 3), op.add)
-    ts(R("s4"), R("s3"), R("rd", 1, 2), 1.0, op.add, op.min)
+    tt(R("s1"), R("Yd"), R("Ye"), op.is_equal, R("PL", 16, 18))
+    tc(R("s5"), R("s1"), ind=R("PL", 8, 16))
+    scan(R("s6"), 128, R("s5"), "R4")
+    tt(R("s6", 127, 128), R("s6", 127, 128), R("rd", 2, 3), op.add)
+    ts(R("s4"), R("s6", 3, 128, 4), R("rd", 1, 2), 1.0, op.add, op.min)
     tt(R("s2"), R("JC"), R("s4"), op.mult)
     tt(R("s1"), R("s2"), R("Yd", 0, 32), op.max)
     tc(R("oU"), R("s1"))
     tc(R("inv"), R("iC"), oind=R("oU"))
-    tt(R("GM", 0, C), R("inv", 0, C), R("mk", 0, C), op.mult)
-    scan(R("SB", 0, C), C, R("GM", 0, C))
-    ts(R("NP"), R("SB", 15, C, 16), 256.0, None, op.add)
-    hlist(0)
-    for t in range(4):
-        above(t)
+    hold(R("NP"), C, R("inv", 0, C))
     arrived(0)
-    maps(0)
+    yrep(1)
+    yrep(2)
+    w = dist(R("YR", 0, 512), R("NP"), C)
+    ts(R("MU", 0, 24), w, 256.0, None, op.add)
     renew(0)
     for r in (1, 2):
         score(r, 0)
         score(r, 1)
         layer(r)
         turned(r)
-        send_t(r)
-        for k in range(len(CH)):
-            pack_h(r, k)
-            send_h(r, k)
         if r == 1:
             quant(R("vq"), R("vs"), R("vb"))
         trep(r)
-        if r == 1:
-            yrep(1)
-            yrep(2)
         for t in range(4):
-            if t == 2:
+            if t == 3:
                 hlist(r)
             unpack(r, t)
         for t in range(4):

from concourse.bass import DstId, RemoteDMATransfer
from concourse.mybir import dt, AluOpType, AxisListType, ActivationFunctionType as AF

C = 384
CH = [(0, 192), (192, 384)]
HC = [(0, 128), (128, 384)]
FQ = ["AAAA", "AVVV", "AVVV"]
SCRATCH = {
    "KX": ("sbuf", [128, 32], "int32"), "KF": ("sbuf", [128, 32], "float32"), "tm": ("sbuf", [128, 128], "int32"),
    "AD": ("sbuf", [128, 8], "float32"), "rL": ("sbuf", [128, 16], "float32"), "rA": ("sbuf", [128, 16], "float32"),
    "rK": ("sbuf", [128, 16], "float32"), "rN": ("sbuf", [128, 8], "float32"), "bh": ("sbuf", [128, 16], "float32"),
    "eqm": ("sbuf", [128, 16], "float32"), "sx": ("sbuf", [128, 16], "float32"), "ow": ("sbuf", [128, 16], "float32"),
    "NK": ("sbuf", [128, 8], "float32"), "OH": ("sbuf", [128, 4], "float32"), "H2": ("sbuf", [128, 2], "float32"),
    "iC": ("sbuf", [128, 512], "bfloat16"), "mk": ("sbuf", [128, 512], "bfloat16"), "R0": ("sbuf", [128, 512], "bfloat16"),
    "TB": ("sbuf", [128, 288], "float32"), "MX": ("sbuf", [128, 384], "bfloat16"), "SF": ("sbuf", [128, 384], "float32"),
    "R4": ("sbuf", [128, 128], "bfloat16"), "GA": ("sbuf", [128, 384], "bfloat16"), "SB2": ("sbuf", [128, 224], "bfloat16"),
    "PL": ("sbuf", [128, 18], "uint16"), "PS": ("sbuf", [128, 128], "bfloat16"), "Ye": ("sbuf", [128, 32], "float32"),
    "s5": ("sbuf", [128, 128], "float32"), "s6": ("sbuf", [128, 128], "float32"),
    "ULi": ("sbuf", [128, 8], "int32"),
    "UL": ("sbuf", [128, 8], "uint16"), "JC": ("sbuf", [128, 32], "float32"), "hf": ("sbuf", [128, 128], "bfloat16"),
    "idn": ("sbuf", [128, 128], "bfloat16"), "EB": ("sbuf", [128, 2048], "bfloat16"),
    "eq": ("sbuf", [128, 512], "float8_e4m3fn_x4"), "es": ("sbuf", [128, 512], "uint8"),
    "seI": ("sbuf", [128, 24], "int32"), "paI": ("sbuf", [128, 24], "int32"), "paU": ("sbuf", [128, 24], "uint16"),
    "slI": ("sbuf", [128, 24], "int32"), "sh": ("sbuf", [128, 24], "float32"), "sb": ("sbuf", [128, 24], "float32"),
    "sw": ("sbuf", [128, 24], "float32"), "s24": ("sbuf", [128, 24], "float32"), "stU": ("sbuf", [128, 24], "uint16"),
    "xb": ("sbuf", [128, 1536], "bfloat16"), "ub": ("sbuf", [128, 512], "bfloat16"),
    "vb": ("sbuf", [128, 512], "bfloat16"), "wq": ("sbuf", [128, 512], "float8_e4m3fn_x4"), "wp": ("sbuf", [128, 512], "uint8"),
    "uq": ("sbuf", [128, 128], "float8_e4m3fn_x4"), "us": ("sbuf", [128, 128], "uint8"),
    "upq": ("sbuf", [128, 128], "float8_e4m3fn_x4"), "ups": ("sbuf", [128, 128], "uint8"),
    "vq": ("sbuf", [128, 128], "float8_e4m3fn_x4"), "vs": ("sbuf", [128, 128], "uint8"),
    "Nc": ("sbuf", [128, 784], "bfloat16"), "LT": ("sbuf", [128, 8], "uint16"), "LL": ("sbuf", [128, 32], "uint16"),
    "ys": ("sbuf", [128, 8], "float32"), "st4": ("sbuf", [128, 8], "float32"), "t4": ("sbuf", [128, 8], "float32"),
    "rd": ("sbuf", [128, 8], "float32"), "GM": ("sbuf", [128, 512], "bfloat16"), "SB": ("sbuf", [128, 512], "bfloat16"),
    "YU": ("sbuf", [128, 34], "uint16"), "Yd": ("sbuf", [128, 40], "float32"), "s1": ("sbuf", [128, 32], "float32"),
    "s2": ("sbuf", [128, 32], "float32"), "s3": ("sbuf", [128, 32], "float32"), "s4": ("sbuf", [128, 32], "float32"),
    "oU": ("sbuf", [128, 32], "uint16"), "inv": ("sbuf", [128, 1024], "bfloat16"), "NP": ("sbuf", [128, 24], "uint16"),
    "sg": ("sbuf", [128, 400], "bfloat16"), "C0": ("sbuf", [128, 272], "bfloat16"), "C1": ("sbuf", [128, 272], "bfloat16"),
    "SC": ("sbuf", [128, 272], "bfloat16"), "P1": ("sbuf", [128, 128], "bfloat16"), "P4": ("sbuf", [128, 128], "bfloat16"),
    "TU": ("sbuf", [128, 96], "uint16"), "Tr": ("sbuf", [128, 512], "bfloat16"),
    "HL": ("sbuf", [128, 72], "uint16"), "yL": ("sbuf", [128, 96], "uint16"), "tL": ("sbuf", [128, 96], "uint16"),
    "YR": ("sbuf", [128, 1536], "bfloat16"), "Z": ("sbuf", [128, 512], "bfloat16"), "MU": ("sbuf", [128, 72], "uint16"),
    "mr": ("sbuf", [128, 384], "float32"),
    "xq": ("sbuf", [128, 1536], "float8_e4m3fn_x4"), "xs": ("sbuf", [128, 1536], "uint8"), "hb": ("sbuf", [128, 1536], "bfloat16"),
    "hq": ("sbuf", [128, 1152], "float8_e4m3fn_x4"), "hs": ("sbuf", [128, 1152], "uint8"),
    "hL": ("sbuf", [128, 1152], "float8_e4m3fn_x4"), "hP": ("sbuf", [128, 1152], "uint8"),
    "fb": ("sbuf", [128, 1536], "bfloat16"), "bb": ("sbuf", [128, 1536], "bfloat16"), "ab": ("sbuf", [128, 1536], "bfloat16"),
    "xn": ("sbuf", [128, 1536], "bfloat16"), "yb": ("sbuf", [128, 384], "float32"),
}
for _k in range(8):
    SCRATCH["ps%d" % _k] = ("psum", [128, 512], "float32")
SEMAPHORES = (["cV", "cA", "cT", "cG", "loc"] + ["d%d" % k for k in range(24)] + ["ay%d" % k for k in range(3)]
              + ["at%d" % k for k in range(3)] + ["as%d" % k for k in range(3)]
              + ["ah%d_%d" % (r, k) for r in range(3) for k in range(len(HC))])


def rank_program(g, core, T, topo):
    rank = T.rank_of(core)
    if rank is None:
        return
    op = AluOpType
    eng = {"V": g.vector, "A": g.scalar, "T": g.tensor, "G": g, "Y": g.sync}
    cnt = {q: 0 for q in eng}
    know = {q: {} for q in eng}
    snap = {}
    acc = {}
    dmas = []
    loc = [0]

    def R(n, a=0, b=None, s=1):
        return (n, a, SCRATCH[n][1][1] if b is None else b, s)

    def v(r):
        n, a, b, s = r
        return T[n][:, a:b] if s == 1 else T[n][:, a:b:s]

    def meet(a, b):
        if a[3] == b[3] and a[3] > 1 and (a[1] - b[1]) % a[3]:
            return False
        return a[1] < b[2] and b[1] < a[2]

    def wait(q, tok):
        if know[q].get(tok[0], 0) >= tok[1]:
            return
        eng[q].wait_ge(T.sem[tok[0]], tok[1])
        for k, n in list(snap.get(tok, {}).items()) + [tok]:
            know[q][k] = max(know[q].get(k, 0), n)

    def order(q, rd, wr, dma=False):
        need = {}
        for r, w in [(r, False) for r in rd] + [(r, True) for r in wr]:
            bank = r[0].startswith("ps")
            for r0, w0, q0, tok in acc.get(r[0], []):
                if bank:
                    if q0 == q and not (w0 or w) or (q0 == q and q == "T"):
                        continue
                elif not (w or w0) or not meet(r, r0):
                    continue
                need[tok[0]] = max(need.get(tok[0], 0), tok[1])
        for k in sorted(need):
            wait(q, (k, need[k]))

    def record(q, rd, wr, tok):
        snap[tok] = dict(know[q])
        for r, w in [(r, False) for r in rd] + [(r, True) for r in wr]:
            l = acc.setdefault(r[0], [])
            if w and r[3] == 1:
                l[:] = [e for e in l if not (r[1] <= e[0][1] and e[0][2] <= r[2])]
            if w and r[0].startswith("ps"):
                l[:] = []
            l.append((r, w, q, tok))

    def emit(q, fn, rd, wr):
        rd = [r for r in rd if isinstance(r, tuple)]
        order(q, rd, wr)
        cnt[q] += 1
        fn().then_inc(T.sem["c" + q], 1)
        record(q, rd, wr, ("c" + q, cnt[q]))

    def dma(q, out, in_, rd, wr):
        order(q, rd, wr, True)
        s = "d%d" % len(dmas)
        dmas.append((q, s))
        eng[q].dma_start(out, in_).then_inc(T.sem[s], 16)
        record(q, rd, wr, (s, 16))

    def sc(x):
        return v(x) if isinstance(x, tuple) else x

    def tt(out, a, b, o, ind=None):
        emit("V", lambda: g.vector.tensor_tensor(v(out), v(a).indirect(v(ind)) if ind else v(a), v(b), o), [a, b, ind], [out])

    def ts(out, a, s1, s2, o1, o2=None):
        if o2 is None:
            emit("V", lambda: g.vector.tensor_scalar(v(out), v(a), sc(s1), None, o1), [a, s1], [out])
        else:
            emit("V", lambda: g.vector.tensor_scalar(v(out), v(a), sc(s1), sc(s2), o1, o2), [a, s1, s2], [out])

    def tc(out, a, ind=None, oind=None):
        emit("V", lambda: g.vector.tensor_copy(v(out).indirect(v(oind)) if oind else v(out), v(a).indirect(v(ind)) if ind else v(a)),
             [a, ind, oind], [out])

    def act(out, a, f=AF.Copy, ind=None, **k):
        emit("A", lambda: g.scalar.activation(v(out), v(a).indirect(v(ind)) if ind else v(a), f, **k), [a, ind], [out])

    def fill(out, x):
        emit("V", lambda: g.vector.memset(v(out), x), [], [out])

    def total(out, a):
        emit("V", lambda: g.vector.tensor_reduce(v(out), v(a), AxisListType.X, op.add), [a], [out])

    def scan(out, n, a, z="R0"):
        emit("V", lambda: g.vector.tensor_tensor_scan(v(out), v(R(z, 0, n)), v(a), 0.0, op.mult, op.add), [R(z, 0, n), a], [out])

    def hold(out, n, a):
        f = R("SF", 0, n)
        emit("V", lambda: g.vector.tensor_tensor_scan(v(f), v(R("MX", 0, n)), v(a), 0.0, op.add, op.max), [R("MX", 0, n), a], [f])
        ts(out, R("SF", 15, n, 16), R("AD", 6, 7), None, op.add)

    def quant(q, s, a):
        emit("V", lambda: g.vector.quantize_mx(v(q), v(s), v(a)), [a], [q, s])

    def mm(bank, n, lq, ls, rq, rs):
        o = R("ps%d" % bank, 0, n)
        emit("T", lambda: g.tensor.matmul_mx(v(o), v(lq), v(ls), v(rq), v(rs), True, True), [lq, ls, rq, rs], [o])

    def iota(out, pat, base, cm=0):
        kw = {} if SCRATCH[out[0]][2] == "int32" else {"allow_small_or_imprecise_dtypes": True}
        emit("G", lambda: g.iota(v(out), pat, base, cm, **kw), [], [out])

    rest = []

    def slip():
        if rest:
            rest.pop(0)()

    def dist(win, ind, n, o="SB", a=0):
        tt(R("GM", 0, n), win, R("mk", 0, n), op.mult, ind)
        slip()
        scan(R(o, a, a + n), n, R("GM", 0, n))
        slip()
        return R(o, a + 15, a + n, 16)

    def b8(r):
        return v(r).bitcast(dt.uint8)

    dma("Y", v(R("seI")), T.se[:, :], [], [R("seI")])
    dma("Y", v(R("ub")), T.u[:, :], [], [R("ub")])
    for a, b in CH:
        dma("Y", v(R("xb", 4 * a, 4 * b)), T.x[:, 4 * a:4 * b], [], [R("xb", 4 * a, 4 * b)])
    dma("Y", b8(R("wq")), T.wc[:, :], [], [R("wq")])
    dma("Y", v(R("wp")), T.ws[:, :], [], [R("wp")])
    dma("Y", v(R("vb")), T.v[:, :], [], [R("vb")])
    part = [T.cores[rank ^ s] for s in (1, 2, 3)]

    def engs(a, b):
        return topo.engines(a, b)

    def some(e):
        m = 0
        for k in e:
            m |= 1 << k
        return m
    cut = [(0, 4), (4, 6), (6, 8)]
    for r in range(3):
        n = len(engs(part[r], core))
        acc.setdefault("yL", []).append((R("yL", 32 * r, 32 * r + 32), True, "R", ("ay%d" % r, cut[r][1] - cut[r][0])))
        acc.setdefault("tL", []).append((R("tL", 32 * r, 32 * r + 32), True, "R", ("at%d" % r, n)))
        acc.setdefault("hP", []).append((R("hP", C * r, C * r + C), True, "R", ("as%d" % r, n)))
        for k, (a, b) in enumerate(HC):
            acc.setdefault("hL", []).append((R("hL", C * r + a, C * r + b), True, "R", ("ah%d_%d" % (r, k), n)))

    iota(R("KX"), [[0, 32]], 0, 1)
    iota(R("iC", 0, 384), [[1, 384]], -256)
    iota(R("tm"), [[0, 8], [1, 16]], 0, -1)
    iota(R("ULi"), [[16, 8]], 0)
    for a, n in ((0, 2), (2, 2), (4, 4), (8, 8)):
        iota(R("rL", a, a + n), [[1, n]], 0 if a else -1)
        iota(R("rA", a, a + n), [[0, n]], 256 // max(a, 1))
        iota(R("rK", a, a + n), [[0, n]], 2 * max(a, 1))
    for a, n, w in ((0, 2, 1), (2, 2, 4), (4, 1, 16)):
        iota(R("rN", a, a + n), [[w, n]], w)
    iota(R("iC", 384, 512), [[1, 128]], 128)
    fill(R("hf"), 0.5)
    fill(R("R0"), 1.0)
    fill(R("R0", 0, 512, 16), 0.0)
    fill(R("PS"), 0.0)
    fill(R("TB", 0, 128), -241.0)
    fill(R("TB", 128, 288), -240.0)
    fill(R("R4"), 1.0)
    fill(R("R4", 0, 128, 4), 0.0)
    for a, b, m in ((0, 2, 0), (2, 4, 1), (4, 8, 3), (8, 16, 7), (16, 17, 15), (17, 18, 1)):
        ts(R("KX", a, b), R("KX", a, b), m, None, op.bitwise_and)
    for k in range(1, 4):
        w = R("KX", 16 + 2 ** k, 16 + 2 ** (k + 1))
        ts(w, w, k, 1, op.logical_shift_right, op.bitwise_and)
    tc(R("KF"), R("KX"))
    q_ = R("KF", 16, 17)

    def bit(k):
        return R("KF", 16 + 2 ** k, 17 + 2 ** k)
    ts(R("AD", 0, 1), q_, 0.0, None, op.is_equal)
    ts(R("tm"), R("tm"), 15, None, op.bitwise_and)
    ts(R("mk", 0, 128), R("tm"), 0.0, None, op.is_equal)
    tc(R("LT", 0, 1), bit(0))
    act(R("Nc", 0, 768, 2), R("iC", 0, 384))
    act(R("Nc", 1, 768, 2), R("iC", 0, 384))
    act(R("AD", 1, 2), R("AD", 0, 1), AF.Identity, scale=768.0)
    act(R("AD", 2, 3), R("AD", 0, 1), AF.Identity, scale=128.0, bias=256.0)
    for k in range(1, 4):
        act(R("AD", 2 + k, 3 + k), bit(k), AF.Identity, bias=512.0)
    act(R("mk", 128, 256), R("mk", 0, 128))
    act(R("mk", 256, 512), R("mk", 0, 256))
    act(R("AD", 6, 7), q_, AF.Identity, scale=512.0, bias=-7424.0)
    act(R("MX"), R("mk", 0, 384), AF.Identity, scale=-33280.0, bias=512.0)
    act(R("ys", 0, 1), q_, AF.Identity, scale=0.0, bias=-256.0)
    act(R("H2", 0, 1), q_, AF.Identity, scale=0.0, bias=256.0)
    act(R("H2", 1, 2), q_, AF.Identity, scale=0.0, bias=256.5)
    act(R("sg", 384, 400), R("KF", 0, 16), AF.Identity, scale=0.0, bias=1.0)
    act(R("Yd", 32, 40), R("KF", 0, 8), AF.Identity, scale=0.0, bias=1000.0)
    act(R("bh"), R("KF", 16, 32), AF.Identity, bias=-0.5)
    for m, n, w in ((0, 1, 8.0), (1, 2, 4.0), (3, 4, 2.0), (7, 8, 1.0)):
        act(R("C0", 16 * m, 16 * (m + n)), R("mk", 16 * m, 16 * (m + n)), AF.Identity, scale=w)
    ts(R("paI"), R("seI"), 1, None, op.arith_shift_right)
    ts(R("slI"), R("seI"), 1, None, op.bitwise_and)
    tc(R("paU"), R("paI"))
    ts(R("sh"), R("slI"), -1.0, 0.5, op.mult, op.add)
    tt(R("sb"), R("seI"), R("sh"), op.add)
    ts(R("sb", 0, 1), R("sb", 0, 1), R("AD", 1, 2), None, op.add)
    fill(R("EB"), 0.0)

    def score(r, k):
        a, b = CH[k]
        bank = (0, 7)[k]
        mm(bank, b - a, R("upq"), R("ups"), R("xq", C * r + a, C * r + b), R("xs", C * r + a, C * r + b))
        act(R("sg", a, b), R("ps%d" % bank, 0, b - a), AF.Sign, bias=2.0 ** -93)

    def pack_x(r, src):
        for k, (a, b) in enumerate(CH):
            quant(R("xq", C * r + a, C * r + b), R("xs", C * r + a, C * r + b), R(src, 4 * a, 4 * b))

    HB = [[1, 2, 3, 4], [5, 6, 0, 7]]

    def layer(r):
        for k, (a, b) in enumerate(HC):
            for t in range(4):
                mm(HB[k][t], b - a, R("wq", 128 * t, 128 * t + 128), R("wp", 128 * t, 128 * t + 128),
                   R("xq", C * r + a, C * r + b), R("xs", C * r + a, C * r + b))
                act(R("hb", 4 * a + t, 4 * b, 4), R("ps%d" % HB[k][t], 0, b - a), scale=0.03125)

    def pack_h(r, k):
        a, b = HC[k]
        quant(R("hq", C * r + a, C * r + b), R("hs", C * r + a, C * r + b), R("hb", 4 * a, 4 * b))

    def remote(dst, out, in_, rd, sem):
        order("G", rd, [], True)
        rid, pid, _ = topo.addr(dst)
        g.remote_dma(out_ap=out, in_ap=in_, remote_sem=T.sem[sem], local_sem=T.sem.loc, pid=pid, routing_id=rid,
                     dma_engine_mask=topo.mask(core, dst))
        loc[0] += len(engs(core, dst))

    def send_h(r, k):
        a, b = C * r + HC[k][0], C * r + HC[k][1]
        remote(part[r], b8(R("hL", a, b)), b8(R("hq", a, b)), [R("hq", a, b)], "ah%d_%d" % (r, k))

    def send_s(r):
        w = (C * r, C * r + C)
        remote(part[r], v(R("hP", *w)), v(R("hs", *w)), [R("hs", *w)], "as%d" % r)

    def send_t(r):
        w = (32 * r, 32 * r + 32)
        remote(part[r], v(R("tL", *w)), v(R("TU", *w)), [R("TU", *w)], "at%d" % r)

    def send_y():
        order("G", [R("YU", 0, 32)], [], True)
        tr = []
        for r in range(3):
            rid, pid, _ = topo.addr(part[r])
            tr.append(RemoteDMATransfer(dst_ids=[DstId(rid=rid, pnc=pid)], remote_sem=T.sem["ay%d" % r], src=v(R("YU", 0, 32)),
                                        dma_engine_mask=some(engs(core, part[r])[cut[r][0]:cut[r][1]]), dst=v(R("yL", 32 * r, 32 * r + 32))))
            loc[0] += cut[r][1] - cut[r][0]
        g.remote_dma_fused(tr, local_sem=T.sem.loc)

    emit("G", lambda: g.affine_select(v(R("idn")), v(R("hf")), [[-1, 128]], op.is_equal, 0.0, 0, 1), [R("hf")], [R("idn")])
    def table(n, o, s, items):
        for a, pat, base in items:
            m = 1
            for _, c in pat:
                m *= c
            iota(R(n, o + s * a, o + s * (a + m - 1) + 1, s), pat, base - 256 if n == "TB" else base)
    one = [[0, 1]]
    table("TB", 0, 4, [(0, [[0, 2], [16, 8]], 127), (23, [[0, 2], [16, 4]], 63), (19, [[0, 2], [16, 2]], 31), (31, one, 271)])
    table("TB", 1, 4, [(0, [[0, 4], [16, 4]], 63), (23, [[0, 4], [16, 2]], 31)])
    table("TB", 2, 4, [(0, [[0, 8], [16, 2]], 31)])
    up = [(0, [[0, 2], [1, 8]], 23), (23, [[0, 2], [1, 4]], 19), (19, [[0, 2], [1, 2]], 17)]
    table("PS", 0, 4, [(0, [[2, 2], [0, 8]], -1), (23, [[2, 2], [0, 4]], -1), (19, [[2, 2], [0, 2]], -1), (17, [[2, 2]], -1), (31, one, 1)])
    table("PS", 1, 4, [(0, [[0, 2], [2, 2], [0, 4]], -1), (23, [[0, 2], [2, 2], [0, 2]], -1), (19, [[0, 2], [2, 2]], -1)])
    table("PS", 2, 4, [(0, [[0, 4], [2, 2], [0, 2]], -1), (23, [[0, 4], [2, 2]], -1)])
    table("PS", 3, 4, [(0, [[0, 8], [2, 2]], -1)])
    table("TB", 128, 4, [(0, [[1, 32]], 0)])
    table("TB", 129, 4, up)
    table("TB", 130, 4, [(0, [[0, 4], [1, 4]], 19), (23, [[0, 4], [1, 2]], 17)])
    table("TB", 131, 4, [(0, [[0, 8], [1, 2]], 17)])
    table("TB", 256, 1, up + [(16, one, 32), (31, one, 32)])
    iota(R("JC"), [[16, 32]], 400, 1)
    for b in range(4):
        act(R("EB", 512 * b + b, 512 * b + 512, 4), R("idn"))

    def yrep(r):
        act(R("YR", 512 * r, 512 * r + 512), R("iC"), ind=R("yL", 32 * r, 32 * r + 32))

    def unpack(r, t):
        mm(1 + t, C, R("eq", 128 * t, 128 * t + 128), R("es", 128 * t, 128 * t + 128), R("xq", C * r, C * r + C), R("xs", C * r, C * r + C))
        if FQ[r][t] == "V":
            tc(R("fb", C * t, C * t + C), R("ps%d" % (1 + t), 0, C))
        else:
            act(R("fb", C * t, C * t + C), R("ps%d" % (1 + t), 0, C))

    def above(t):
        act(R("bb", C * t, C * t + C), R("fb", C * t, C * t + C), ind=R("paU"))

    def level(l):
        n, at, o = 2 << l, (2 << l) - 2, 16 * ((2 << l) - 2)
        w = dist(R("Nc", 0, 768), R("LL", at, at + n), 16 * n, "SB2", o)
        at += n
        ts(R("LL", at, at + n), w, 2.0, 512.0, op.mult, op.add)
        ts(R("LL", at + n, at + 2 * n), w, 2.0, 513.0, op.mult, op.add)

    tc(R("UL"), R("ULi"))
    ts(R("NK", 0, 5), R("rN", 0, 5), q_, -1.0, op.is_gt, op.mult)
    tt(R("eqm"), R("rL"), R("KF", 0, 16), op.is_equal)
    tt(R("OH"), R("NK", 0, 4), R("NK", 1, 5), op.subtract)
    quant(R("uq"), R("us"), R("ub"))
    act(R("ups"), R("us"), ind=R("UL"))
    emit("V", lambda: g.vector.tensor_copy(v(R("upq")).bitcast(dt.uint32), v(R("uq")).bitcast(dt.uint32).indirect(v(R("UL")))),
         [R("uq"), R("UL")], [R("upq")])
    tt(R("sx"), R("bh"), R("rA"), op.mult)
    ts(R("ow"), R("rK"), q_, -1.0, op.is_gt, op.mult)
    tt(R("C0", 240, 256), R("eqm"), R("sx"), op.mult)
    pack_x(0, "xb")
    score(0, 0)
    score(0, 1)
    quant(R("eq"), R("es"), R("EB"))
    tt(R("C0", 256, 272), R("C0", 240, 256), R("ow"), op.mult)
    ts(R("C0", 256, 257), R("AD", 0, 1), -256.0, None, op.mult)
    for t in range(4):
        unpack(0, t)
    layer(0)
    for t in range(4):
        above(t)
    w = dist(R("sg", 0, 400), R("paU"), C)
    tt(R("sw"), w, R("sh"), op.mult)
    tt(R("s24"), R("sb"), R("sw"), op.subtract)
    tc(R("stU"), R("s24"))
    tc(R("Nc"), R("iC", 0, 384), oind=R("stU"))
    for k in range(4):
        tt(R("GM", 0, 16), R("Nc", 0, 768), R("mk", 0, 16), op.mult, R("LT", 2 * k, 2 * k + 1))
        slip()
        total(R("ys", k + 1, k + 2), R("GM", 0, 16))
        slip()
        if k < 3:
            ts(R("LT", 2 * k + 2, 2 * k + 3), R("ys", k + 1, k + 2), 2.0, R("AD", k + 3, k + 4), op.mult, op.add)
        if k == 1:
            pack_h(0, 0)
            pack_h(0, 1)
            send_h(0, 0)
            send_s(0)
            send_h(0, 1)
    ts(R("LL", 0, 2), R("H2"), R("ys", 4, 5), 2.0, op.add, op.mult)
    rest.extend([
        lambda: tt(R("t4", 0, 4), R("OH"), R("ys", 0, 4), op.mult),
        lambda: ts(R("YU", 16, 17), R("ys", 4, 5), 256.0, None, op.add),
    ])
    slip()
    level(0)
    rest.extend([
        lambda: total(R("rd", 0, 1), R("t4", 0, 4)),
        lambda: tt(R("st4", 0, 4), R("ys", 0, 4), R("ys", 1, 5), op.is_equal),
        lambda: ts(R("YU", 31, 32), R("rd", 0, 1), R("AD", 2, 3), None, op.add),
        lambda: total(R("rd", 1, 2), R("st4", 0, 4)),
        lambda: tt(R("t4", 4, 8), R("st4", 0, 4), R("NK", 1, 5), op.mult),
        lambda: ts(R("YU", 32, 33), R("rd", 0, 1), R("AD", 2, 3), None, op.add),
        lambda: total(R("rd", 2, 3), R("t4", 4, 8)),
    ])
    level(1)
    level(2)
    act(R("GA", 0, 256), R("Nc", 0, 768), ind=R("LL", 14, 30))
    ts(R("YU", 17, 31), R("SB2", 15, 224, 16), 256.0, None, op.add)
    while rest:
        slip()
    hold(R("YU", 0, 16), 256, R("GA", 0, 256))
    send_y()
    hold(R("PL"), 288, R("TB"))
    yrep(0)

    def turned(r):
        c0, c1 = ("C0", "C1") if r == 1 else ("C1", "C0")
        tt(R(c1), R("sg"), R(c0), op.mult, R("YU", 16, 33))
        scan(R("SC"), 272, R(c1))
        pack_h(r, 0)
        tt(R("P1"), R("SC"), R("PS"), op.mult, R("PL", 0, 8))
        scan(R("P4"), 128, R("P1"), "R4")
        ts(R("TU", 32 * r, 32 * r + 32), R("P4", 3, 128, 4), 256.0, R("SC", 255, 256), op.add, op.add)
        pack_h(r, 1)
        send_h(r, 0)
        send_t(r)
        send_s(r)
        send_h(r, 1)

    def trep(r):
        act(R("Tr"), R("iC"), ind=R("TU", 32 * r, 32 * r + 32))

    def hlist(r):
        w = dist(R("Tr"), R("NP"), C)
        ts(R("HL", 24 * r, 24 * r + 24), w, 256.0, None, op.add)

    def arrived(r):
        for k, (a, b) in enumerate(HC):
            for t in range(4):
                bk = HB[1 - k][t]
                mm(bk, b - a, R("eq", 128 * t, 128 * t + 128), R("es", 128 * t, 128 * t + 128),
                   R("hL", C * r + a, C * r + b), R("hP", C * r + a, C * r + b))
                act(R("ab", C * t + a, C * t + b), R("ps%d" % bk, 0, b - a))

    def maps(r):
        tc(R("Z"), R("YR", 512 * r, 512 * r + 512), oind=R("tL", 32 * r, 32 * r + 32))
        w = dist(R("Z"), R("HL", 24 * r, 24 * r + 24), C)
        ts(R("MU", 24 * r, 24 * r + 24), w, 256.0, None, op.add)

    def renew(r):
        for t in range(4):
            tt(R("xn", t, 1536, 4), R("ab", C * t, C * t + C), R("bb", C * t, C * t + C), op.add, R("MU", 24 * r, 24 * r + 24))
        pack_x(r + 1, "xn")


    tc(R("Yd", 0, 32), R("YU", 0, 32))
    tc(R("Ye"), R("YU", 0, 32))
    tt(R("s1"), R("Yd"), R("Ye"), op.is_equal, R("PL", 16, 18))
    tc(R("s5"), R("s1"), ind=R("PL", 8, 16))
    scan(R("s6"), 128, R("s5"), "R4")
    tt(R("s6", 127, 128), R("s6", 127, 128), R("rd", 2, 3), op.add)
    ts(R("s4"), R("s6", 3, 128, 4), R("rd", 1, 2), 1.0, op.add, op.min)
    tt(R("s2"), R("JC"), R("s4"), op.mult)
    tt(R("s1"), R("s2"), R("Yd", 0, 32), op.max)
    tc(R("oU"), R("s1"))
    tc(R("inv"), R("iC"), oind=R("oU"))
    hold(R("NP"), C, R("inv", 0, C))
    arrived(0)
    yrep(1)
    yrep(2)
    w = dist(R("YR", 0, 512), R("NP"), C)
    ts(R("MU", 0, 24), w, 256.0, None, op.add)
    renew(0)
    for r in (1, 2):
        score(r, 0)
        score(r, 1)
        layer(r)
        turned(r)
        if r == 1:
            quant(R("vq"), R("vs"), R("vb"))
        trep(r)
        for t in range(4):
            if t == 3:
                hlist(r)
            unpack(r, t)
        for t in range(4):
            above(t)
        arrived(r)
        maps(r)
        if r == 2:
            act(R("mr"), R("Z"), AF.Identity, ind=R("HL", 48, 72), bias=256.0)
            dma("Y", T.im[:, :], T.mr[0:128:16, 0:C], [R("mr")], [])
        renew(r)
    for k, (a, b) in enumerate(CH):
        q3, s3 = R("xq", 3 * C + a, 3 * C + b), R("xs", 3 * C + a, 3 * C + b)
        mm((0, 7)[k], b - a, R("vq"), R("vs"), q3, s3)
        act(R("yb", a, b), R("ps%d" % (0, 7)[k], 0, b - a))
        dma("Y", T.oc[:, 4 * a:4 * b], b8(q3), [q3], [])
        dma("A", T.y[:, a:b], v(R("yb", a, b)), [R("yb", a, b)], [])
    for k in range(4):
        dma("Y", T.osc[4 * k:4 * k + 4, :], T.xs[32 * k:32 * k + 4, 3 * C:4 * C], [R("xs", 3 * C, 4 * C)], [])
    for q, s in dmas:
        wait(q, (s, 16))
    for q in ("V", "A", "T", "G"):
        g.wait_ge(T.sem["c" + q], cnt[q])
    g.wait_ge(T.sem.loc, loc[0])
